import numpy as np, ml_dtypes
CORES = [48,51,52,55]
N = 4
import mx_ref
BF = ml_dtypes.bfloat16
def entries(a):
    return np.ascontiguousarray(a.T).reshape(-1)
def table(e):
    return np.ascontiguousarray(np.reshape(e, (-1, 16)).T).astype(np.int32)
def cols(t, e):
    v = np.concatenate([t.reshape(128, -1, 4), np.zeros((128, 1, 4), BF)], axis=1)
    return np.ascontiguousarray(v[:, e]).reshape(128, -1)
def cut(t, i, w=512):
    return t[:, w * i:w * i + w]
def pick(q, e):
    c = np.concatenate([q[0].reshape(128, -1, 4), np.zeros((128, 1, 4), np.uint8)], axis=1); s = np.concatenate([q[1], np.ones((16, 1), np.uint8)], axis=1)
    return (np.ascontiguousarray(c[:, e].reshape(128, -1)), np.ascontiguousarray(s[:, e]))
def join(*qs):
    return (np.concatenate([q[0] for q in qs], axis=1), np.concatenate([q[1] for q in qs], axis=1))
def put(q, e, v):
    c, s = q[0].reshape(128, -1, 4).copy(), q[1].copy(); c[:, e] = v[0].reshape(128, -1, 4); s[:, e] = v[1]
    return (c.reshape(128, -1), s)
def pk(c, s):
    return (np.ascontiguousarray(c), mx_ref.live(s))
def emit(q):
    return q[0], q[1]
def decode(q):
    o = []
    for b in range(4):
        e = np.zeros((128, 128, 4), np.float32); e[np.arange(128), np.arange(128), b] = 1
        o.append(mx_ref.matmul(mx_ref.quantize(e.reshape(128, 512).astype(BF)), q))
    return np.stack(o, axis=2).reshape(128, -1)
def f(rng, *shape):
    return mx_ref.flush((rng.standard_normal(shape, dtype=np.float32) * np.exp2(rng.integers(-2, 3, shape[:-1] + (1,)))).astype(BF))
def wide(rng, *shape, cols=0):
    v = rng.standard_normal(shape, dtype=np.float32) * np.exp2(rng.integers(-12, 13, shape)).astype(np.float32)
    if cols: v *= np.repeat(np.exp2(rng.integers(-cols, cols + 1, shape[:-2] + (1, shape[-1] // 4))) * (rng.random(shape[:-2] + (1, shape[-1] // 4)) > 0.0625), 4, axis=-1).astype(np.float32)
    return mx_ref.flush(v.astype(BF))
P, A, C, E, KP = 384, 32, 16, 8, 4
LC, M = 160, 3
def clean(v):
    v = np.array(v, np.float32)
    v[np.abs(v) < np.float32(2.0 ** -16)] = 0
    return v.astype(BF)
def lists(rng, full=False, own=False):
    out = []
    for r in range(N):
        pool = np.stack([P * q + rng.permutation(P)[:LC] for q in range(N)])
        must = np.zeros(0, int)
        if full: must = rng.permutation(pool[(r + 1 + rng.permutation(N - 1)[:M]) % N].reshape(-1))
        if own: must = P * r + rng.permutation(P)[:A * (C - 4)]
        rows = []
        for i in range(A):
            a = must[i::A]
            b = rng.permutation(np.setdiff1d(pool, a))[:C - a.size]
            rows.append(rng.permutation(np.concatenate([a, b])))
        out.append(table(np.concatenate(rows)))
    return {"cd": np.stack(out)}
def clusters(rng, n, low, high, noise):
    m = f(rng, 128, 4 * n).astype(np.float32).reshape(128, n, 4)
    h = rng.integers(0, n, (N, P))
    tb = np.stack([m[:, h[q]].reshape(128, -1) for q in range(N)]) + noise * f(rng, N, 128, 4 * P).astype(np.float32)
    a = low + (high - low) * rng.random((N, A, n))
    x = np.einsum("png,rin->rpig", m, a).reshape(N, 128, 4 * A) + noise * f(rng, N, 128, 4 * A).astype(np.float32)
    return {"tb": clean(tb), "x": clean(x), "w": f(rng, N, 128, 512)}
def setup_inputs(rng):
    return {**clusters(rng, 8, 0.2, 1.0, 0.5), **lists(rng)}
def setup_inputs_alike(rng):
    return {**clusters(rng, 3, 0.3, 0.7, 0.25), **lists(rng, full=True)}
def setup_inputs_one(rng):
    o, m, n = 0, min(A, LC // KP), P // KP
    kind = rng.permutation(P) % KP
    part = np.arange(128) // (128 // KP)
    tb = f(rng, N, 128, 4 * P).astype(np.float32).reshape(N, 128, P, 4) * np.float32(0.0625)
    tb[o] = (4 + 4 * rng.random((128, P, 4))) * (part[:, None] == kind[None, :])[:, :, None]
    order = np.stack([rng.permutation(np.flatnonzero(kind == k)) for k in range(KP)])
    out = []
    for r in range(N):
        size, at = (A, 0) if r == o else (m, A + m * (r - int(r > o)))
        big = P * o + order[:, (at + np.arange(A) % size) % n]
        pool = rng.permutation(np.concatenate([P * q + rng.permutation(P)[:LC] for q in range(N) if q != o]))
        rest = pool[:A * (C - KP)].reshape(A, C - KP)
        out.append(table(np.concatenate([rng.permutation(v) for v in np.concatenate([big.T, rest], axis=1)])))
    return {"tb": clean(tb.reshape(N, 128, 4 * P)), "x": clean(1 + rng.random((N, 128, 4 * A))), "w": f(rng, N, 128, 512), "cd": np.stack(out)}
def setup_inputs_ties(rng):
    m = clean(f(rng, 128, 12)).astype(np.float32).reshape(128, 3, 4)
    h = rng.integers(0, 3, (N, P))
    i = np.arange(A)
    k = np.where(i // 3 % 2 == 0, 1.0, 2.0)[None, :, None]
    tb = clean(np.stack([m[:, h[q]].reshape(128, -1) for q in range(N)])).reshape(N, 128, P, 4)
    x = clean(np.stack([(m[:, (i + r) % 3] * k).reshape(128, -1) for r in range(N)])).reshape(N, 128, A, 4)
    cd = lists(rng, own=True)["cd"]
    top = np.arange(128) < 64
    x[:, :, A - 2] = np.where(top, 4.0, 1.0).astype(BF)[None, :, None]
    x[:, :, A - 1] = np.where(top, -1.0, -4.0).astype(BF)[None, :, None]
    for r in range(N):
        g = rng.permutation(P)[:C + 1]
        g[:3] = np.sort(g[:3])
        tb[r][:, g[0]] = BF(-0.0)
        tb[r][:, g[1]] = BF(0.0)
        tb[r][:, g[2]] = np.array([1.0, -1.0, 1.0, -1.0]).astype(BF)[None, :]
        tb[r][:, g[3:]] = clean((1 + rng.random((128, C - 2, 4))) * np.where(top, -1.0, 1.0)[:, None, None])
        e = np.array(entries(cd[r])).reshape(A, C)
        e[A - 2] = P * r + rng.permutation(np.delete(g, 1))
        e[A - 1] = P * r + rng.permutation(np.delete(g, 0))
        cd[r] = table(e)
    return {"tb": tb.reshape(N, 128, 4 * P), "x": x.reshape(N, 128, 4 * A), "w": f(rng, N, 128, 512), "cd": cd}
def setup_inputs_shared(rng):
    place = np.stack([rng.permutation(P) for q in range(N)])
    tb = f(rng, N, 128, 4 * P).astype(np.float32).reshape(N, 128, P, 4) * np.float32(0.0625)
    part = np.arange(128) // (128 // KP)
    big = np.zeros((N, KP), int)
    for g in range(N):
        for k in range(KP):
            o = (g + k) % N
            tb[o, :, place[o, k]] = (4 + 4 * rng.random((128, 4))) * (part == k)[:, None]
            big[g, k] = P * o + place[o, k]
    out = []
    for r in range(N):
        pool = np.concatenate([P * q + rng.permutation(place[q, KP:])[:LC - KP] for q in range(N)])
        at = rng.integers(0, r + 1, A)
        at[0], at[A - 1] = 0, r
        out.append(table(np.concatenate([rng.permutation(np.concatenate([big[g], rng.permutation(pool)[:C - KP]])) for g in at])))
    return {"tb": clean(tb.reshape(N, 128, 4 * P)), "x": clean(1 + rng.random((N, 128, 4 * A))), "w": f(rng, N, 128, 512), "cd": np.stack(out)}
def setup_inputs_spread(rng):
    return {"tb": clean(wide(rng, N, 128, 4 * P, cols=6)), "x": clean(wide(rng, N, 128, 4 * A, cols=6)), "w": f(rng, N, 128, 512), **lists(rng)}
def check_inputs(d):
    b = []
    for k, low in (("tb", -16), ("x", -16), ("w", -30)):
        v = np.abs(d[k].astype(np.float32))
        if not (np.isfinite(v).all() and ((v == 0) | (v >= 2.0 ** low) & (v <= 2.0 ** 30)).all()): b.append("a value of " + k)
    for r in range(N):
        e = entries(d["cd"][r])
        if e.min() < 0 or e.max() >= N * P:
            b.append("cd: a number out of range")
            continue
        if any(len(set(v.tolist())) < C for v in e.reshape(A, C)): b.append("cd: a candidate twice at one point")
        n = np.bincount(np.unique(e) // P, minlength=N)
        n[r] = 0
        if n.max() > LC: b.append("cd: too many columns of one other rank")
    return b
def chosen(every, x, cd):
    kept = np.full((N, A, KP), -1)
    for r in range(N):
        e = entries(cd[r])
        t = cols(every, e)
        v = mx_ref.quantize(t)
        points = mx_ref.quantize(cols(x[r], np.concatenate([np.arange(A), np.full(128 - A, -1)])))
        s = mx_ref.matmul(points, v) + np.float32(0)
        g = np.concatenate([mx_ref.matmul(mx_ref.quantize(np.ascontiguousarray(cut(t, j))), v) for j in range(C * A // 128)]) + np.float32(0)
        for i in range(A):
            at = np.arange(C * i, C * i + C)
            best = at[np.lexsort((e[at], -s[i, at]))[:E]]
            mine = []
            for c in best:
                if len(mine) < KP and all(s[i, c] > g[c, k] for k in mine): mine.append(c)
            kept[r, i, :len(mine)] = e[mine]
    return kept
def reference(tb, x, w, cd):
    every = np.concatenate([tb[q] for q in range(N)], axis=1)
    kept = chosen(every, x, cd)
    y = np.zeros((N, 128, KP * A), np.float32)
    oc, osc = np.zeros((N, 128, 4 * P), np.uint8), np.zeros((N, 16, P), np.uint8)
    for r in range(N):
        y[r] = mx_ref.matmul(mx_ref.quantize(w[r]), mx_ref.quantize(cols(every, kept[r].reshape(-1))))
    dx = [decode(mx_ref.quantize(x[r])).reshape(128, A, 4) for r in range(N)]
    half = np.float32(0.5)
    for q in range(N):
        v = mx_ref.quantize(tb[q])
        m = decode(v).reshape(128, P, 4)
        named = np.zeros(P, bool)
        for r in range(N):
            for i in range(A):
                for c in kept[r, i]:
                    j = c - P * q
                    if 0 <= j < P and not named[j]:
                        m[:, j] = m[:, j] * half + dx[r][:, i] * half
                        named[j] = True
        at = np.flatnonzero(named)
        new = mx_ref.quantize(np.ascontiguousarray(m.reshape(128, -1).astype(BF)))
        oc[q], osc[q] = emit(put(v, at, pick(new, at)))
    return {"y": y, "kp": np.ascontiguousarray(kept.transpose(0, 2, 1)).astype(np.float32), "oc": oc, "osc": osc}

@@ -1,0 +1,452 @@
+from concourse.bass import DstId, RemoteDMATransfer
+from concourse.mybir import dt, AluOpType, AxisListType, ActivationFunctionType
+
+N, P, A, C, LC = 4, 384, 32, 16, 160
+UB = 32
+UR = UB + P
+UW = UR + 3 * LC
+MO = 3 * P
+MW = MO + 4 * P
+
+F32, BF, I32, U16, U8, F8 = "float32", "bfloat16", "int32", "uint16", "uint8", "float8_e4m3fn_x4"
+SCRATCH = {}
+for _d, _names in (
+    (BF, "tbt:1536 xt:512 wt:512 et:2048 nt:1536"),
+    (F8, "vq:384 xq:128 wq:128 eq:512 xa:128 uc:896 pk:480 ex:1024 kq:128 qp:384 mg:768 oq:384"),
+    (U8, "vqs:384 xqs:128 wqs:128 eqs:512 xas:128 ucs:896 pks:480 exs:1024 kqs:128 qps:384 mgs:768 oqs:384"),
+    (I32, "kci:56"), (U16, "bl:8 xl:32 pl:2"), (BF, "ones:16"),
+    (F32, "kcf:512 idt:1552 key:512 keyi:512"),
+    (I32, "cdi:32"), (U16, "off:64 lst:10 lnd:32 ls:32"), (BF, "mk0:2688 mk1:2688 mo:384 pc:384 js:2304 jv:1536"), (F32, "cdp:32 acc:16"),
+    (F32, "zf:416 g1:32 zr:1024 zt:1024 z1:32 z2:32 sf:32 sc:16 nc:16 n1:8 nr:64 tie0:64 tie:64"), (U16, "og:64 sw:32 nl:4"),
+    (F32, "cs:1024 cg:512 ss:128 gg:64 w2:128 a2:64 bb:64 rk:4 l2a:8 l2b:8 t1:128 t1t:128 t2:640 t2t:256 ff:240 tmp:64"), (U16, "l1:4 l2:8"),
+    (F32, "k8:8 cn:8 ck:8 ck4:32 nn4:32 sl4:32 knm:64 kn:8 lx:64 lxt:64 nl2:8 nlf:16 kpr:32 kpt:32 yt:128"), (U16, "kl:8 ksl:8 kla:24"),
+    (F32, "vr:512 abo:384 ab:1176 rp:32 rpt:32 rd:64 rdt:64 lc:6 lnf:24 sl0:24 sl1:24"), (U16, "ln:24 sl:24"),
+):
+    for _n in _names.split():
+        SCRATCH[_n.split(":")[0]] = ("sbuf", [128, int(_n.split(":")[1])], _d)
+PART = {}
+for _d, _names in (
+    ("kcf", "pf:8 cq:8 ca:8 s16:10 sv:10 sg:10 im:64 iv:64 iw:64 dg:64 dh:64 c2a:8 c2b:8 c2e:8 c2f:8 c2d:8 c2g:8 c2:8 mj0:8 mj:8 cc:4 cd0:4 jc0:24 jc:24"),
+    ("kci", "ip:2 ib:8 ix:32 it:8"),
+):
+    _c = 0
+    for _n in _names.split():
+        PART[_n.split(":")[0]] = (_d, _c, int(_n.split(":")[1]))
+        _c += PART[_n.split(":")[0]][2]
+BANKS = ["pb%d" % _b for _b in range(8)]
+for _n in BANKS:
+    SCRATCH[_n] = ("psum", [128, 512], F32)
+SEMAPHORES = ["ev", "ec", "et_", "ep", "dcd", "dx", "dtb", "dw", "du", "dxa", "dmg", "dz", "dk", "dy", "do0", "do1", "dp0", "dp1",
+              "arx", "arl", "arc", "ark", "loc"]
+
+
+def rank_program(g, core, T, topo):
+    r = T.rank_of(core)
+    if r is None:
+        return
+    O, AF, X = AluOpType, ActivationFunctionType, AxisListType.X
+    eng = {"v": g.vector, "s": g.scalar, "t": g.tensor, "p": g, "y": g.sync}
+    semof = {"v": "ev", "s": "ec", "t": "et_", "p": "ep"}
+    count = {}
+    known = {k: {} for k in eng}
+    log = {}
+
+    def R(name, c0=0, c1=None, p0=0, p1=128, st=1):
+        name, base, n = PART.get(name, (name, 0, SCRATCH[name][1][1] if name in SCRATCH else 0))
+        c0, c1 = base + c0, base + (n if c1 is None else c1)
+        ap = T[name][p0:p1, c0:c1] if st == 1 else T[name][p0:p1, c0:c1:st]
+        return {"n": name, "c0": c0, "c1": c1, "p0": p0, "p1": p1, "st": st, "ap": ap}
+
+    def meet(a, b):
+        if a["p1"] <= b["p0"] or b["p1"] <= a["p0"] or a["c1"] <= b["c0"] or b["c1"] <= a["c0"]:
+            return False
+        return not (a["st"] == b["st"] and a["st"] > 1 and (a["c0"] - b["c0"]) % a["st"])
+
+    def need(q, outs, ins, skip=None):
+        todo = {}
+        for kind, regs in (("w", outs), ("r", ins)):
+            for x in regs:
+                bank = x["n"] in BANKS
+                for y, k, tok in log.get(x["n"], []):
+                    if (skip is not None and tok[3] == skip) or known[q].get(tok[0], 0) >= tok[1]:
+                        continue
+                    if bank:
+                        hit = tok[0] != semof.get(q) or (q != "t" and meet(x, y) and "w" in (kind, k))
+                    else:
+                        hit = "w" in (kind, k) and meet(x, y)
+                    if hit and (tok[0] not in todo or todo[tok[0]][1] < tok[1]):
+                        todo[tok[0]] = tok
+        for s in sorted(todo):
+            tok = todo[s]
+            if known[q].get(s, 0) >= tok[1]:
+                continue
+            eng[q].wait_ge(T.sem[s], tok[1])
+            for a, b in list(tok[2].items()) + [(s, tok[1])]:
+                known[q][a] = max(known[q].get(a, 0), b)
+
+    def note(q, outs, ins, sem, val, tag=None):
+        tok = (sem, val, dict(known[q]) if q else {}, tag)
+        for k, regs in (("w", outs), ("r", ins)):
+            for x in regs:
+                log.setdefault(x["n"], []).append((x, k, tok))
+
+    def op(q, call, outs, ins):
+        need(q, outs, ins)
+        s = semof[q]
+        count[s] = count.get(s, 0) + 1
+        call().then_inc(T.sem[s], 1)
+        note(q, outs, ins, s, count[s])
+
+    def u8(x):
+        return x["ap"].bitcast(dt.uint8) if SCRATCH[x["n"]][2] == F8 else x["ap"]
+
+    def dma(q, o, i, sem, total):
+        outs, ins = [x for x in (o,) if isinstance(x, dict)], [x for x in (i,) if isinstance(x, dict)]
+        need(q, outs, ins, skip=sem)
+        eng[q].dma_start(u8(o) if outs else o, u8(i) if ins else i).then_inc(T.sem[sem], 16)
+        count[sem] = count.get(sem, 0) + 16
+        note(q, outs, ins, sem, 16 * total, tag=sem)
+
+    def memset(a, c):
+        op("v", lambda: g.vector.memset(a["ap"], c), [a], [])
+
+    def copy(o, i, q="v"):
+        if q == "v":
+            op("v", lambda: g.vector.tensor_copy(o["ap"], i["ap"]), [o], [i])
+        else:
+            op("s", lambda: g.scalar.activation(o["ap"], i["ap"], AF.Copy), [o], [i])
+
+    def tt(o, a, b, f):
+        op("v", lambda: g.vector.tensor_tensor(o["ap"], a["ap"], b["ap"], f), [o], [a, b])
+
+    def ts(o, a, s1, s2, f1, f2=None):
+        ins = [a] + [s for s in (s1, s2) if isinstance(s, dict)]
+        v1 = s1["ap"] if isinstance(s1, dict) else s1
+        v2 = s2["ap"] if isinstance(s2, dict) else s2
+        if f2 is None:
+            op("v", lambda: g.vector.tensor_scalar(o["ap"], a["ap"], v1, None, f1), [o], ins)
+        else:
+            op("v", lambda: g.vector.tensor_scalar(o["ap"], a["ap"], v1, v2, f1, f2), [o], ins)
+
+    def red(o, a, f):
+        op("v", lambda: g.vector.tensor_reduce(o["ap"], a["ap"], X, f), [o], [a])
+
+    def scan(o, a):
+        op("v", lambda: g.vector.tensor_tensor_scan(o["ap"], a["ap"], a["ap"], 0.0, O.add, O.max), [o], [a])
+
+    def act(o, a, f, bias=None, scale=1.0, acc=None):
+        kw = {"scale": scale}
+        if bias is not None:
+            kw["bias"] = bias["ap"] if isinstance(bias, dict) else bias
+        if acc is not None:
+            kw["accum_out"] = acc["ap"]
+        op("s", lambda: g.scalar.activation(o["ap"], a["ap"], f, **kw), [o] + ([acc] if acc else []), [a] + ([bias] if isinstance(bias, dict) else []))
+
+    def turn(o, a):
+        op("v", lambda: g.vector.transpose(o["ap"], a["ap"]), [o], [a])
+
+    def gather(o, win, off, q="v"):
+        if q == "v":
+            op("v", lambda: g.vector.tensor_copy(o["ap"], win["ap"].indirect(off["ap"])), [o], [win, off])
+        else:
+            op("s", lambda: g.scalar.activation(o["ap"], win["ap"].indirect(off["ap"]), AF.Copy), [o], [win, off])
+
+    def scatter(win, off, i):
+        op("v", lambda: g.vector.tensor_copy(win["ap"].indirect(off["ap"]), i["ap"]), [win], [off, i])
+
+    def pick(cn, o0, o1, wn, w1, off):
+        o, w = R(cn, o0, o1), R(wn, 0, w1)
+        op("v", lambda: g.vector.tensor_copy(o["ap"].bitcast(dt.uint32), w["ap"].bitcast(dt.uint32).indirect(off["ap"])), [o], [w, off])
+        gather(R(cn + "s", o0, o1), R(wn + "s", 0, w1), off, "s")
+
+    def quant(cn, c0, c1, tile):
+        o, s = R(cn, c0, c1), R(cn + "s", c0, c1)
+        op("v", lambda: g.vector.quantize_mx(o["ap"], s["ap"], tile["ap"]), [o, s], [tile])
+
+    def mm(bank, n, a, a0, b, b0, b1, start=True, stop=True):
+        o, l, ls, m, ms = R(bank, 0, n), R(a, a0, a0 + 128), R(a + "s", a0, a0 + 128), R(b, b0, b1), R(b + "s", b0, b1)
+        op("t", lambda: g.tensor.matmul_mx(o["ap"], l["ap"], ls["ap"], m["ap"], ms["ap"], start, stop), [o], [l, ls, m, ms])
+
+    def iota(name, pattern, base, cm, c0=0, c1=None):
+        o = R(name, c0, c1)
+        kw = {"allow_small_or_imprecise_dtypes": True} if SCRATCH[o["n"]][2] == F32 else {}
+        op("p", lambda: g.iota(o["ap"], pattern, base, cm, **kw), [o], [])
+
+    others = [q for q in range(N) if q != r]
+    at = {q: k for k, q in enumerate(others)}
+    here = {q: (r if r < q else r - 1) for q in others}
+
+    def send(srcs, dsts, sem, turned):
+        need("p", [], srcs)
+        tr = []
+        for k, q in enumerate(others):
+            e = topo.engines(core, T.cores[q])
+            m = len(e) // 4
+            k4 = (k + turned) % 4
+            rid, pid, _s = topo.addr(T.cores[q])
+            tr.append(RemoteDMATransfer(dst_ids=[DstId(rid=rid, pnc=pid)], dma_engine_mask=sum(1 << n for n in e[k4 * m:k4 * m + m]),
+                                        remote_sem=T.sem[sem], src=u8(srcs[k]), dst=u8(dsts[k])))
+            count["loc"] = count.get("loc", 0) + m
+            count[sem] = count.get(sem, 0) + m
+        g.remote_dma_fused(tr, local_sem=T.sem.loc)
+
+    for k in range(8):
+        dma("ys"[k % 2], R("cdi", 0, 32, 16 * k, 16 * k + 16), T.cd[:, :], "dcd", 8)
+    dma("y", R("xt", 0, 128), T.x[:, :], "dx", 1)
+    dma("s", R("tbt"), T.tb[:, :], "dtb", 1)
+    dma("y", R("wt"), T.w[:, :], "dw", 1)
+
+    iota("ip", [[1, 1]], 0, 1, 0, 1)
+    iota("s16", [[16, 10]], 0, 0)
+    iota("c2b", [[32, 4], [16, 2]], 512, 0)
+    iota("c2a", [[1 - 1024, 4], [0, 2]], 0, 0)
+    iota("im", [[0, 4], [1, 16]], 0, 0)
+    iota("iv", [[32, 4], [0, 16]], 0, 0)
+    iota("mj0", [[0, 2], [1, 4]], 0, 0)
+    iota("ib", [[128, 8]], 0, 1)
+    iota("ix", [[1, 4], [4, 8]], 0, 0)
+    iota("cd0", [[-32, 3]], -P * r, -1, 0, 3)
+    iota("jc0", [[16, 24]], 0, 0)
+    memset(R("mk0", MO, MO + P), 0.0)
+    memset(R("mk1", MO, MO + P), 0.0)
+    memset(R("xt", 128, 512), 0.0)
+    memset(R("ones"), 1.0)
+    p = R("ip", 0, 1)
+    for k, (sh, msk) in enumerate(((0, 15), (4, 1), (1, 3), (4, 7), (0, 3), (5, 3))):
+        ts(R("it", k, k + 1), p, sh, msk, O.logical_shift_right, O.bitwise_and)
+    for a in range(4):
+        memset(R("cq", 2, 3, 32 * a, 32 * a + 32), float(0 if a == r else UR + LC * at[a] - 1))
+    copy(R("pf", 0, 6), R("it", 0, 6))
+    lcol, hcol, bcol, gcol, p3, acol = [R("pf", k, k + 1) for k in range(6)]
+    ts(R("cq", 0, 1), acol, float(-P), float(MO), O.mult, O.add)
+    ts(R("sv"), R("s16"), lcol, None, O.add)
+    ts(R("cq", 1, 2), acol, float(-P), 16.0, O.mult, O.add)
+    ts(R("sg"), R("sv"), 0.5, None, O.add)
+    ts(R("ca", 0, 1), hcol, 16.0, None, O.mult)
+    ts(R("ca", 1, 2), hcol, -508.0, None, O.mult)
+    ts(R("ca", 2, 3), hcol, -1.0, 1.0, O.mult, O.add)
+    ts(R("ca", 3, 4), hcol, 32.0, None, O.mult)
+    ts(R("ca", 4, 5), acol, -64.0, None, O.mult)
+    ts(R("ca", 5, 6), hcol, -32.0, 32.0, O.mult, O.add)
+
+    quant("xq", 0, 128, R("xt"))
+    for s, k in (("", 0), ("s", 3)):
+        send([R("xq" + s, 0, 32)] * 3, [R("xa" + s, 32 * r, 32 * r + 32)] * 3, "arx", k)
+    for s in ("", "s"):
+        dma("y", R("uc" + s, 0, 32), R("xq" + s, 32, 64), "dz", 2)
+        dma("y", R("xa" + s, 32 * r, 32 * r + 32), R("xq" + s, 0, 32), "dxa", 2)
+    iota("idt", [[1, 1552]], -1, 0)
+
+    ts(R("off", 0, 64, st=2), R("cdi"), R("cq", 0, 1), None, O.add)
+    for i in range(A):
+        scatter(R("mk%d" % (i % 2)), R("off", 2 * i, 2 * i + 1), R("ones"))
+    tt(R("mo"), R("mk0", MO, MO + P), R("mk1", MO, MO + P), O.max)
+    pc = R("pc")
+    scan(pc, R("mo"))
+    pl_ = R("pc", 0, P - 1)
+    for k in range(6):
+        act(R("js", P * k, P * k + P - 1), pl_, AF.Sign, bias=R("sg", k, k + 1), scale=-1.0, acc=R("acc", k, k + 1))
+    for k in range(6, 10):
+        ts(R("jv", P * (k - 6), P * (k - 6) + P - 1), pl_, R("sv", k, k + 1), None, O.is_le)
+    for k in range(6, 10):
+        red(R("acc", k, k + 1), R("jv", P * (k - 6), P * (k - 6) + P - 1), O.add)
+    copy(R("lst", 6, 10), R("acc", 6, 10))
+    ts(R("lst", 0, 6), R("acc", 0, 6), 0.5, 0.5 * (P - 1), O.mult, O.add)
+    send([R("lst")] * 3, [R("lnd", 10 * here[q], 10 * here[q] + 10) for q in others], "arl", 0)
+
+    iota("t1", [[0, 128]], 0, 0)
+    iota("t2", [[0, 640]], 0, 0)
+    quant("vq", 0, P, R("tbt"))
+    for s in ("", "s"):
+        dma("y", R("uc" + s, UB, UR), R("vq" + s), "du", 2)
+        dma("y", R("mg" + s, 0, P), R("vq" + s), "dmg", 2)
+    memset(R("zf", 0, 16), 0.0)
+    memset(R("zf", 400, 416), 0.0)
+    act(R("zf", 16, 400), pc, AF.Identity, bias=R("cq", 2, 3))
+    copy(R("zf", 16, 400, 32 * r, 32 * r + 32), R("idt", UB + 1, UB + 1 + P, 32 * r, 32 * r + 32), "s")
+    for j in range(4):
+        copy(R("cdp", 8 * j, 8 * j + 8), R("cdi", j, 32, st=4))
+    ts(R("g1"), R("cdp"), R("cq", 1, 2), 15.0, O.add, O.max)
+    ts(R("pl", 0, 1), bcol, 8.0, gcol, O.mult, O.add)
+    ts(R("og", 0, 64, st=2), R("g1"), 400.0, None, O.min)
+    ts(R("og", 1, 64, st=2), R("g1"), 400.0, None, O.min)
+    gather(R("zr"), R("zf"), R("og"), "s")
+    gather(R("nc"), R("cdp"), R("pl", 0, 1))
+    copy(R("bl"), R("ib"))
+    copy(R("xl"), R("ix"))
+    ts(R("n1"), R("nc", 0, 8), 1.0, None, O.add)
+    ts(R("iw"), R("iv"), R("ca", 0, 1), None, O.add)
+    ts(R("dh"), R("im"), lcol, None, O.is_equal)
+    copy(R("nl"), R("n1", 0, 8, st=2))
+    ts(R("c2e"), R("c2a"), R("ca", 1, 2), None, O.add)
+    ts(R("c2f"), R("c2b"), lcol, None, O.add)
+    gather(R("nr"), R("idt"), R("nl"))
+    tt(R("dg"), R("dh"), R("iw"), O.mult)
+    ts(R("mj"), R("mj0"), p3, None, O.is_equal)
+
+    note(None, [R("lnd", 0, 30)], [], "arl", count["arl"])
+    for a in range(4):
+        copy(R("ls", 0, 30, 32 * a, 32 * a + 32), R("lnd", 0, 30, 32 * r, 32 * r + 32))
+    pick("pk", 0, 3 * LC, "vq", P, R("ls", 0, 30))
+    for s, k in (("", 0), ("s", 3)):
+        send([R("pk" + s, LC * k_, LC * k_ + LC) for k_ in range(3)], [R("uc" + s, UR + LC * here[q], UR + LC * here[q] + LC) for q in others], "arc", k)
+
+    iota("rp", [[0, 32]], 0, 0)
+    iota("kpr", [[0, 32]], 0, 0)
+    for k, q in enumerate([r] + others):
+        iota("keyi", [[4, 8], [1, 4], [0, 4]], 32 * q, 0, 128 * k, 128 * k + 128)
+    for k in range(2):
+        act(R("et", 1024 * k, 1024 * k + 1024), R("idt", 0, 1024), AF.Identity, bias=0.5, scale=0.0)
+    et = R("et")
+    op("p", lambda: g.affine_select(et["ap"], et["ap"], [[1, 4], [-1, 512]], O.is_equal, 0.0, 0, 4), [et], [et])
+
+    turn(R("zt"), R("zr"))
+    tt(R("z1", 0, 32, 0, 64), R("zt", 0, 1024, 0, 64, 32), R("zt", 0, 1024, 64, 128, 32), O.add)
+    tt(R("z2", 0, 32, 0, 32), R("z1", 0, 32, 0, 32), R("z1", 0, 32, 32, 64), O.add)
+    for a in range(4):
+        copy(R("sf", 0, 32, 32 * a, 32 * a + 32), R("z2", 0, 32, 0, 32))
+    for j in range(4):
+        pick("ex", 256 * j + 128, 256 * j + 256, "xq", 128, R("xl", 8 * j, 8 * j + 8))
+        if j == 0:
+            copy(R("sw"), R("sf"))
+            gather(R("sc"), R("sf"), R("pl", 0, 1))
+    for j in range(4):
+        ts(R("tie0", 16 * j, 16 * j + 16), R("nr", 16 * j, 16 * j + 16), R("nc", 2 * j, 2 * j + 1), None, O.is_lt)
+    tt(R("c2d"), R("c2e"), R("c2f"), O.subtract)
+    tt(R("tie"), R("tie0"), R("dg"), O.add)
+    ts(R("c2g", 0, 8, st=2), R("c2d", 0, 8, st=2), R("ca", 2, 3), None, O.mult)
+    ts(R("c2g", 1, 8, st=2), R("c2d", 1, 8, st=2), hcol, None, O.mult)
+    ts(R("cc", 0, 3), R("cd0", 0, 3), R("ca", 4, 5), None, O.add)
+    tt(R("c2"), R("c2g"), R("c2f"), O.add)
+    ts(R("jc"), R("jc0"), lcol, None, O.add)
+
+    note(None, [R(n, UR, UW) for n in ("uc", "ucs")], [], "arc", count["arc"])
+    for j in range(4):
+        pick("ex", 256 * j, 256 * j + 128, "uc", UW, R("sw", 8 * j, 8 * j + 8))
+    for j in range(4):
+        mm(BANKS[4 + j], 128, "ex", 256 * j + 128, "ex", 256 * j, 256 * j + 128)
+        mm(BANKS[j], 256, "ex", 256 * j, "ex", 256 * j, 256 * j + 256)
+    for j in range(4):
+        copy(R("cs", 128 * j, 128 * j + 128), R(BANKS[4 + j], 0, 128), "s")
+        copy(R("cs", 512 + 128 * j, 640 + 128 * j), R(BANKS[j], 128, 256))
+    for j in range(4):
+        copy(R("cg", 128 * j, 128 * j + 128), R(BANKS[j], 0, 128), "s")
+    act(R("key"), R("keyi"), AF.Copy, scale=1.0 / 256)
+    gather(R("ss"), R("cs"), R("bl"))
+    sr, so = R("ss", 0, 64), R("ss", 64, 128)
+    tt(R("a2"), sr, so, O.is_equal)
+    tt(R("w2", 0, 128, st=2), sr, so, O.is_gt)
+    tt(R("w2", 1, 128, st=2), R("a2"), R("tie"), O.mult)
+    gather(R("gg"), R("cg"), R("bl", 0, 4))
+    for j in range(4):
+        red(R("rk", j, j + 1), R("w2", 32 * j, 32 * j + 32), O.add)
+    tt(R("bb"), R("gg"), so, O.is_ge)
+    copy(R("l1"), R("rk"))
+    ts(R("l2a", 0, 8, st=2), R("rk"), R("ca", 5, 6), None, O.mult)
+    ts(R("l2a", 1, 8, st=2), R("rk"), R("ca", 3, 4), None, O.mult)
+    scatter(R("t1"), R("l1"), R("bb"))
+    tt(R("l2b"), R("l2a"), R("c2"), O.add)
+    copy(R("t1", 15, 128, st=16), R("n1"))
+    copy(R("t1", 14, 128, st=16), R("sc", 0, 8))
+    copy(R("l2"), R("l2b"))
+    turn(R("t1t"), R("t1"))
+    scatter(R("t2"), R("l2"), R("t1t"))
+    turn(R("t2t"), R("t2", 0, 256))
+    tt(R("ff"), R("t2t", 0, 240), R("t2t", 16, 256), O.add)
+    for k in range(4):
+        copy(R("nn4", 8 * k, 8 * k + 8), R("ff", 15, 240, st=32), "s")
+    for k in range(4):
+        copy(R("sl4", 8 * k, 8 * k + 8), R("ff", 14, 240, st=32), "s")
+    memset(R("k8", 0, 1), 1.0)
+    for u in range(1, 7):
+        t, d = R("tmp", 8 * u, 8 * u + 7 - u), R("ff", 32 * (u + 1), 240, st=32)
+        ts(t, R("ff", 32 * (u + 1) + u, 240, st=32), R("ff", 32 * u, 32 * u + 1), None, O.is_gt)
+        tt(d, d, t, O.max)
+    ts(R("k8", 1, 8), R("ff", 32, 240, st=32), -1.0, 1.0, O.mult, O.add)
+    scan(R("cn"), R("k8"))
+    tt(R("ck"), R("cn"), R("k8"), O.mult)
+    for k in range(4):
+        ts(R("ck4", 8 * k, 8 * k + 8), R("ck"), float(k + 1), None, O.is_equal)
+
+    def rows(k, src):
+        tt(R("knm", 32 * k, 32 * k + 32), R("ck4"), R(src), O.mult)
+        for m in range(4):
+            red(R("kn", 4 * k + m, 4 * k + m + 1), R("knm", 32 * k + 8 * m, 32 * k + 8 * m + 8), O.add)
+        for m in range(4):
+            ts(R("lx", 32 * k + m, 32 * k + 32, st=4), R("mj"), R("kn", 4 * k + m, 4 * k + m + 1), None, O.mult)
+        turn(R("lxt", 32 * k, 32 * k + 32), R("lx", 32 * k, 32 * k + 32))
+        for h in range(2):
+            red(R("nl2", 2 * k + h, 2 * k + h + 1), R("lxt", 32 * k + 4 * h, 32 * k + 4 * h + 4), O.add)
+
+    def spread(o, c0, w, i, i0):
+        for a in range(4):
+            for b in range(4):
+                copy(R(o, c0 + w * a, c0 + w * a + w, 32 * b, 32 * b + 32), R(i, i0, i0 + w, 32 * a, 32 * a + 32), "vs"[b % 2])
+    rows(0, "nn4")
+    spread("nlf", 0, 2, "nl2", 0)
+    copy(R("kl"), R("nlf", 0, 8))
+    send([R("kl")] * 3, [R("kla", 8 * here[q], 8 * here[q] + 8) for q in others], "ark", 0)
+
+    def rowsum(o, off, k):
+        op("v", lambda: g.vector.tensor_tensor(o["ap"], R("idt")["ap"].indirect(off["ap"]), k["ap"], O.add), [o], [R("idt"), off, k])
+    rowsum(R("vr", 0, 128), R("kl"), R("key", 0, 128))
+    for k in range(3):
+        act(R("abo", 128 * k, 128 * k + 128), R("vr", 0, 128), AF.Abs, bias=R("cc", k, k + 1))
+    quant("eq", 0, 512, R("et"))
+    quant("wq", 0, 128, R("wt"))
+    ts(R("kpr", 0, 4), R("kn", 0, 4), -1.0, None, O.add)
+    for ch in range(2):
+        for b in range(4):
+            mm(BANKS[4 * ch + b], 192, "eq", 128 * b, "vq", 192 * ch, 192 * ch + 192, True, False)
+    turn(R("kpt"), R("kpr"))
+    for a in range(4):
+        dma("y", T.kp[:, 8 * a:8 * a + 8], R("kpt", 0, 8, 32 * a, 32 * a + 4), "dk", 4)
+    for k in range(3):
+        red(R("ab", 392 * k + 384, 392 * k + 385), R("abo", 128 * k, 128 * k + 128), O.min)
+
+    note(None, [R("kla")], [], "ark", count["ark"])
+    for s in (0, 192):
+        rowsum(R("vr", 128 + s, 320 + s), R("kla", s // 16, s // 16 + 12), R("key", 128 + s, 320 + s))
+        for k in range(3):
+            act(R("ab", 392 * k + s, 392 * k + s + 192), R("vr", 128 + s, 320 + s), AF.Abs, bias=R("cc", k, k + 1))
+    for k in range(3):
+        red(R("rp", k, k + 1), R("ab", 392 * k, 392 * k + 385), O.min)
+    turn(R("rpt"), R("rp"))
+    for c in range(4):
+        s = 16 * (c // 2)
+        copy(R("rd", 16 * c, 16 * c + 16), R("rpt", s, s + 16), "vs"[c % 2])
+    turn(R("rdt"), R("rd"))
+    copy(R("lc", 0, 6, st=2), R("rdt", 0, 3))
+    copy(R("lc", 1, 6, st=2), R("rdt", 32, 35))
+    spread("lnf", 0, 6, "lc", 0)
+    ts(R("ln"), R("lnf"), 256.0, 127.0, O.mult, O.min)
+
+    note(None, [R("xa" + s, 32 * q, 32 * q + 32) for q in others for s in ("", "s")], [], "arx", count["arx"])
+    for ch in range(2):
+        pick("qp", 192 * ch, 192 * ch + 192, "xa", 128, R("ln", 12 * ch, 12 * ch + 12))
+    for ch in range(2):
+        for b in range(4):
+            mm(BANKS[4 * ch + b], 192, "eq", 128 * b, "qp", 192 * ch, 192 * ch + 192, False, True)
+    ts(R("sl0"), R("lnf"), 0.5, 384.0, O.is_lt, O.mult)
+    rows(1, "sl4")
+    tt(R("sl1"), R("sl0"), R("jc"), O.add)
+    copy(R("sl"), R("sl1"))
+    for ch in range(2):
+        for b in range(4):
+            copy(R("nt", 768 * ch + b, 768 * ch + 768, st=4), R(BANKS[4 * ch + b], 0, 192), "vs"[b % 2])
+        quant("mg", P + 192 * ch, P + 192 * ch + 192, R("nt", 768 * ch, 768 * ch + 768))
+        if ch == 0:
+            spread("nlf", 8, 2, "nl2", 2)
+            copy(R("ksl"), R("nlf", 8, 16))
+            pick("kq", 0, 128, "uc", UW, R("ksl"))
+            mm(BANKS[0], 128, "wq", 0, "kq", 0, 128)
+        pick("oq", 192 * ch, 192 * ch + 192, "mg", 2 * P, R("sl", 12 * ch, 12 * ch + 12))
+        dma("y", T.oc[:, 768 * ch:768 * ch + 768], R("oq", 192 * ch, 192 * ch + 192), "do%d" % ch, 1)
+        for k in range(4):
+            dma("sy"[k % 2], T.osc[4 * k:4 * k + 4, 192 * ch:192 * ch + 192], R("oqs", 192 * ch, 192 * ch + 192, 32 * k, 32 * k + 4), "dp%d" % ch, 4)
+        if ch == 0:
+            copy(R("yt"), R(BANKS[0], 0, 128), "s")
+            dma("s", T.y[:, :], R("yt"), "dy", 1)
+
+    for s in sorted(count):
+        g.wait_ge(T.sem[s], count[s])

@@ -7,36 +7,42 @@ UR = UB + P
 UW = UR + 3 * LC
 MO = 3 * P
 MW = MO + 4 * P
+DB = P
+EX = 272
 
 F32, BF, I32, U16, U8, F8 = "float32", "bfloat16", "int32", "uint16", "uint8", "float8_e4m3fn_x4"
 SCRATCH = {}
 for _d, _names in (
     (BF, "tbt:1536 xt:512 wt:512 et:2048 nt:1536"),
-    (F8, "vq:384 xq:128 wq:128 eq:512 xa:128 uc:896 pk:480 ex:1024 kq:128 qp:384 mg:768 oq:384"),
-    (U8, "vqs:384 xqs:128 wqs:128 eqs:512 xas:128 ucs:896 pks:480 exs:1024 kqs:128 qps:384 mgs:768 oqs:384"),
-    (I32, "kci:56"), (U16, "bl:8 xl:32 pl:2"), (BF, "ones:16"),
-    (F32, "kcf:512 idt:1552 key:512 keyi:512"),
-    (I32, "cdi:32"), (U16, "off:64 lst:10 lnd:32 ls:32"), (BF, "mk0:2688 mk1:2688 mo:384 pc:384 js:2304 jv:1536"), (F32, "cdp:32 acc:16"),
-    (F32, "zf:416 g1:32 zr:1024 zt:1024 z1:32 z2:32 sf:32 sc:16 nc:16 n1:8 nr:64 tie0:64 tie:64"), (U16, "og:64 sw:32 nl:4"),
-    (F32, "cs:1024 cg:512 ss:128 gg:64 w2:128 a2:64 bb:64 rk:4 l2a:8 l2b:8 t1:128 t1t:128 t2:640 t2t:256 ff:240 tmp:64"), (U16, "l1:4 l2:8"),
-    (F32, "k8:8 cn:8 ck:8 ck4:32 nn4:32 sl4:32 knm:64 kn:8 lx:64 lxt:64 nl2:8 nlf:16 kpr:32 kpt:32 yt:128"), (U16, "kl:8 ksl:8 kla:24"),
-    (F32, "vr:512 abo:384 ab:1176 rp:32 rpt:32 rd:64 rdt:64 lc:6 lnf:24 sl0:24 sl1:24"), (U16, "ln:24 sl:24"),
+    (F8, "vq:384 xq:128 wq:128 eq:512 xa:160 uc:896 pk:480 ex:1088 kq:128 qp:384 mg:768 oq:384"),
+    (U8, "vqs:384 xqs:128 wqs:128 eqs:512 xas:160 ucs:896 pks:480 exs:1088 kqs:128 qps:384 mgs:768 oqs:384"),
+    (I32, "kci:96"), (U16, "bl:8 xl:40 pl:2 rl:24 hv:4"), (BF, "ones:16 eye:128"),
+    (F32, "kcf:512 idt:1552 key:256 keyi:256 cv:192 zz:128"),
+    (I32, "cdh:16 cdi:32"), (U16, "off:32 wl:12 lst:10 lnd:30 ls:30"), (BF, "mk0:2688 mk1:2688 tm:768 m1:24"),
+    (F32, "req:192 x0:32 xt0:32 wn:1152 wnt:160 lr:32 ld:64 ldt:64"),
+    (F32, "cdp:32 zp:12 zrep:384 zf:416 gx:128 zr:512 zt:512 z1:32 z2:128 sf:32 sc:16 nc:16 n1:24 nr:64 tie:64"), (U16, "og:32 sw:32 nl:4"),
+    (F32, "cs:544 cg:512 ss:128 gg:64 dw:64 w2:64 bb:64 rk:8 l2a:8 l2b:8 t1:128 t1t:128 t2:640 t2t:256 cu:64 tmp:64"), (U16, "l1:4 l2:8"),
+    (F32, "pr:128 kpt:32 yr:32 yd:64 ydt:64 yt:128"), (U16, "kl:4 ksl:8 kla:12"),
+    (F32, "vr:256 abo:384 ab:1200 rpt:32 dmn:32 lc:32 lcs:6 sl0:24 sl1:24"), (U16, "ln:24 sl:24"),
 ):
     for _n in _names.split():
         SCRATCH[_n.split(":")[0]] = ("sbuf", [128, int(_n.split(":")[1])], _d)
 PART = {}
 for _d, _names in (
-    ("kcf", "pf:8 cq:8 ca:8 s16:10 sv:10 sg:10 im:64 iv:64 iw:64 dg:64 dh:64 c2a:8 c2b:8 c2e:8 c2f:8 c2d:8 c2g:8 c2:8 mj0:8 mj:8 cc:4 cd0:4 jc0:24 jc:24"),
-    ("kci", "ip:2 ib:8 ix:32 it:8"),
+    ("kcf", "pf:8 cq:8 ca:12 t32:32 tri:32 dc0:12 dc:12 dc1:12 plc:12 c4:4 bo:4 hv0:4 c2a:8 c2b:8 c2e:8 c2f:8 c2d:8 c2g:8 c2:8 cst0:4 cst:4 cc0:6 cc:6 jc0:24 jc:24 mk4:4"),
+    ("kci", "ip:2 ib:4 ix:40 it:8 ir:24"),
+    ("req", "mm:12 tot:1 base:1 sn:12 g1:12 g2:12 g3:12"),
+    ("pr", "al:8 nn:8 sl8:8 mk8:8 ms8:8 cn:8 ck:8 z8:8 y8:8 nlv:1 nls:1 slv:1 kt:1 kv:1 yv:1 kp2:16 kp3:8 kpo:8"),
 ):
     _c = 0
     for _n in _names.split():
         PART[_n.split(":")[0]] = (_d, _c, int(_n.split(":")[1]))
         _c += PART[_n.split(":")[0]][2]
+    assert _c <= SCRATCH[_d][1][1]
 BANKS = ["pb%d" % _b for _b in range(8)]
 for _n in BANKS:
     SCRATCH[_n] = ("psum", [128, 512], F32)
-SEMAPHORES = ["ev", "ec", "et_", "ep", "dcd", "dx", "dtb", "dw", "du", "dxa", "dmg", "dz", "dk", "dy", "do0", "do1", "dp0", "dp1",
+SEMAPHORES = ["ev", "ec", "et_", "ep", "dch", "dcd", "dx", "dtb", "dw", "du", "dxa", "dmg", "dz", "dk", "dy", "do0", "do1", "dp0", "dp1",
               "arx", "arl", "arc", "ark", "loc"]
 
 
@@ -128,19 +134,21 @@ def rank_program(g, core, T, topo):
         else:
             op("v", lambda: g.vector.tensor_scalar(o["ap"], a["ap"], v1, v2, f1, f2), [o], ins)
 
-    def red(o, a, f):
-        op("v", lambda: g.vector.tensor_reduce(o["ap"], a["ap"], X, f), [o], [a])
+    def red(o, a, f, size=False):
+        kw = {"apply_absolute_value": True} if size else {}
+        op("v", lambda: g.vector.tensor_reduce(o["ap"], a["ap"], X, f, **kw), [o], [a])
 
     def scan(o, a):
         op("v", lambda: g.vector.tensor_tensor_scan(o["ap"], a["ap"], a["ap"], 0.0, O.add, O.max), [o], [a])
 
-    def act(o, a, f, bias=None, scale=1.0, acc=None):
+    def act(o, a, f, bias=None, scale=1.0):
         kw = {"scale": scale}
         if bias is not None:
             kw["bias"] = bias["ap"] if isinstance(bias, dict) else bias
-        if acc is not None:
-            kw["accum_out"] = acc["ap"]
-        op("s", lambda: g.scalar.activation(o["ap"], a["ap"], f, **kw), [o] + ([acc] if acc else []), [a] + ([bias] if isinstance(bias, dict) else []))
+        op("s", lambda: g.scalar.activation(o["ap"], a["ap"], f, **kw), [o], [a] + ([bias] if isinstance(bias, dict) else []))
+
+    def lin(o, a, scale=1.0, bias=0.0):
+        act(o, a, AF.Identity, bias=bias, scale=scale)
 
     def turn(o, a):
         op("v", lambda: g.vector.transpose(o["ap"], a["ap"]), [o], [a])
@@ -154,10 +162,12 @@ def rank_program(g, core, T, topo):
     def scatter(win, off, i):
         op("v", lambda: g.vector.tensor_copy(win["ap"].indirect(off["ap"]), i["ap"]), [win], [off, i])
 
-    def pick(cn, o0, o1, wn, w1, off):
+    def pick(cn, o0, o1, wn, w1, off, q="vs"):
         o, w = R(cn, o0, o1), R(wn, 0, w1)
-        op("v", lambda: g.vector.tensor_copy(o["ap"].bitcast(dt.uint32), w["ap"].bitcast(dt.uint32).indirect(off["ap"])), [o], [w, off])
-        gather(R(cn + "s", o0, o1), R(wn + "s", 0, w1), off, "s")
+        if "v" in q:
+            op("v", lambda: g.vector.tensor_copy(o["ap"].bitcast(dt.uint32), w["ap"].bitcast(dt.uint32).indirect(off["ap"])), [o], [w, off])
+        if "s" in q:
+            gather(R(cn + "s", o0, o1), R(wn + "s", 0, w1), off, "s")
 
     def quant(cn, c0, c1, tile):
         o, s = R(cn, c0, c1), R(cn + "s", c0, c1)
@@ -176,277 +186,348 @@ def rank_program(g, core, T, topo):
     at = {q: k for k, q in enumerate(others)}
     here = {q: (r if r < q else r - 1) for q in others}
 
-    def send(srcs, dsts, sem, turned):
-        need("p", [], srcs)
+    def send(pieces, sem, turned=0):
+        need("p", [], [s for _q, s, _d in pieces])
+        parts = 1 if len(pieces) == 1 else 4
         tr = []
-        for k, q in enumerate(others):
+        for k, (q, s, d) in enumerate(pieces):
             e = topo.engines(core, T.cores[q])
-            m = len(e) // 4
-            k4 = (k + turned) % 4
+            m = len(e) // parts
+            k4 = (k + turned) % parts
             rid, pid, _s = topo.addr(T.cores[q])
             tr.append(RemoteDMATransfer(dst_ids=[DstId(rid=rid, pnc=pid)], dma_engine_mask=sum(1 << n for n in e[k4 * m:k4 * m + m]),
-                                        remote_sem=T.sem[sem], src=u8(srcs[k]), dst=u8(dsts[k])))
+                                        remote_sem=T.sem[sem], src=u8(s), dst=u8(d)))
             count["loc"] = count.get("loc", 0) + m
             count[sem] = count.get(sem, 0) + m
         g.remote_dma_fused(tr, local_sem=T.sem.loc)
 
+    def spread(o, n, i, c0, n0, st=1, lo=0, hi=4, qs="vs"):
+        k = 0
+        for a in range(lo, hi):
+            for b in range(4):
+                copy(R(o, n * a, n * a + n, 32 * b, 32 * b + 32), R(i, c0, n0, 32 * a, 32 * a + 32, st), qs[k % len(qs)])
+                k += 1
+
     for k in range(8):
-        dma("ys"[k % 2], R("cdi", 0, 32, 16 * k, 16 * k + 16), T.cd[:, :], "dcd", 8)
+        dma("ys"[k % 2], R("cdh", 0, 16, 16 * k, 16 * k + 16), T.cd[:, 16 * (k % 2):16 * (k % 2) + 16], "dch", 8)
     dma("y", R("xt", 0, 128), T.x[:, :], "dx", 1)
     dma("s", R("tbt"), T.tb[:, :], "dtb", 1)
+    for k in range(8):
+        dma("ys"[k % 2], R("cdi", 0, 32, 16 * k, 16 * k + 16), T.cd[:, :], "dcd", 8)
     dma("y", R("wt"), T.w[:, :], "dw", 1)
 
     iota("ip", [[1, 1]], 0, 1, 0, 1)
-    iota("s16", [[16, 10]], 0, 0)
-    iota("c2b", [[32, 4], [16, 2]], 512, 0)
-    iota("c2a", [[1 - 1024, 4], [0, 2]], 0, 0)
-    iota("im", [[0, 4], [1, 16]], 0, 0)
-    iota("iv", [[32, 4], [0, 16]], 0, 0)
-    iota("mj0", [[0, 2], [1, 4]], 0, 0)
-    iota("ib", [[128, 8]], 0, 1)
-    iota("ix", [[1, 4], [4, 8]], 0, 0)
-    iota("cd0", [[-32, 3]], -P * r, -1, 0, 3)
-    iota("jc0", [[16, 24]], 0, 0)
-    memset(R("mk0", MO, MO + P), 0.0)
-    memset(R("mk1", MO, MO + P), 0.0)
-    memset(R("xt", 128, 512), 0.0)
-    memset(R("ones"), 1.0)
-    p = R("ip", 0, 1)
-    for k, (sh, msk) in enumerate(((0, 15), (4, 1), (1, 3), (4, 7), (0, 3), (5, 3))):
-        ts(R("it", k, k + 1), p, sh, msk, O.logical_shift_right, O.bitwise_and)
-    for a in range(4):
-        memset(R("cq", 2, 3, 32 * a, 32 * a + 32), float(0 if a == r else UR + LC * at[a] - 1))
-    copy(R("pf", 0, 6), R("it", 0, 6))
-    lcol, hcol, bcol, gcol, p3, acol = [R("pf", k, k + 1) for k in range(6)]
-    ts(R("cq", 0, 1), acol, float(-P), float(MO), O.mult, O.add)
-    ts(R("sv"), R("s16"), lcol, None, O.add)
-    ts(R("cq", 1, 2), acol, float(-P), 16.0, O.mult, O.add)
-    ts(R("sg"), R("sv"), 0.5, None, O.add)
-    ts(R("ca", 0, 1), hcol, 16.0, None, O.mult)
-    ts(R("ca", 1, 2), hcol, -508.0, None, O.mult)
-    ts(R("ca", 2, 3), hcol, -1.0, 1.0, O.mult, O.add)
-    ts(R("ca", 3, 4), hcol, 32.0, None, O.mult)
-    ts(R("ca", 4, 5), acol, -64.0, None, O.mult)
-    ts(R("ca", 5, 6), hcol, -32.0, 32.0, O.mult, O.add)
-
-    quant("xq", 0, 128, R("xt"))
-    for s, k in (("", 0), ("s", 3)):
-        send([R("xq" + s, 0, 32)] * 3, [R("xa" + s, 32 * r, 32 * r + 32)] * 3, "arx", k)
-    for s in ("", "s"):
-        dma("y", R("uc" + s, 0, 32), R("xq" + s, 32, 64), "dz", 2)
-        dma("y", R("xa" + s, 32 * r, 32 * r + 32), R("xq" + s, 0, 32), "dxa", 2)
+    iota("t32", [[1, 32]], 0, 0)
+    iota("dc0", [[1, 12]], DB, 0)
+    iota("cv", [[32, 12], [1, 16]], 0, 0)
+    iota("hv0", [[16, 2], [0, 2]], 0, 0)
+    iota("plc", [[32, 12]], UB - 32 * r, 1)
     iota("idt", [[1, 1552]], -1, 0)
+    memset(R("mk0", MO, MO + P), 0.0)
+    p = R("ip", 0, 1)
+    for k, (sh, msk) in enumerate(((0, 15), (4, 1), (0, 7), (4, 7), (0, 3), (5, 3), (0, 31), (1, 3))):
+        ts(R("it", k, k + 1), p, sh, msk, O.logical_shift_right, O.bitwise_and)
+    memset(R("mk1", MO, MO + P), 0.0)
+    copy(R("pf", 0, 8), R("it", 0, 8))
+    lcol, hcol, ecol, gcol, p3, acol, pcol, bcol = [R("pf", k, k + 1) for k in range(8)]
+    memset(R("ones"), 1.0)
+    ts(R("cq", 0, 1), acol, float(-P), float(MO), O.mult, O.add)
+    memset(R("xt", 128, 512), 0.0)
+    ts(R("tri"), R("t32"), pcol, None, O.is_gt)
+    lin(R("ca", 0, 1), hcol, 16.0)
+    lin(R("ca", 6, 7), pcol, 12.0)
+    lin(R("dc"), R("dc0"), 1.0, R("ca", 6, 7))
+    lin(R("cv"), R("cv"), 1.0, R("ca", 0, 1))
+    lin(R("dc1"), R("dc"), 1.0, 1.0)
+    memset(R("wn", 0, LC), 0.0)
+    ts(R("off", 0, 32, st=2), R("cdh"), R("cq", 0, 1), None, O.add)
 
-    ts(R("off", 0, 64, st=2), R("cdi"), R("cq", 0, 1), None, O.add)
-    for i in range(A):
+    def points():
+        quant("xq", 0, 128, R("xt"))
+        for s, k in (("", 0), ("s", 3)):
+            send([(q, R("xq" + s, 0, 32), R("xa" + s, 32 * r, 32 * r + 32)) for q in others], "arx", k)
+        for s in ("", "s"):
+            dma("y", R("uc" + s, 0, 32), R("xq" + s, 32, 64), "dz", 2)
+            dma("y", R("xa" + s, 32 * r, 32 * r + 32), R("xq" + s, 0, 32), "dxa", 4)
+            dma("y", R("xa" + s, 128, 160), R("xq" + s, 32, 64), "dxa", 4)
+
+    for i in range(A // 2):
         scatter(R("mk%d" % (i % 2)), R("off", 2 * i, 2 * i + 1), R("ones"))
-    tt(R("mo"), R("mk0", MO, MO + P), R("mk1", MO, MO + P), O.max)
-    pc = R("pc")
-    scan(pc, R("mo"))
-    pl_ = R("pc", 0, P - 1)
-    for k in range(6):
-        act(R("js", P * k, P * k + P - 1), pl_, AF.Sign, bias=R("sg", k, k + 1), scale=-1.0, acc=R("acc", k, k + 1))
-    for k in range(6, 10):
-        ts(R("jv", P * (k - 6), P * (k - 6) + P - 1), pl_, R("sv", k, k + 1), None, O.is_le)
-    for k in range(6, 10):
-        red(R("acc", k, k + 1), R("jv", P * (k - 6), P * (k - 6) + P - 1), O.add)
-    copy(R("lst", 6, 10), R("acc", 6, 10))
-    ts(R("lst", 0, 6), R("acc", 0, 6), 0.5, 0.5 * (P - 1), O.mult, O.add)
-    send([R("lst")] * 3, [R("lnd", 10 * here[q], 10 * here[q] + 10) for q in others], "arl", 0)
+        if i == 3:
+            points()
+    lin(R("cq", 1, 2), acol, float(-P), 16.0)
+    lin(R("ca", 1, 2), hcol, 4.0 / 256)
+    lin(R("ca", 2, 3), hcol, -1.0, 1.0)
+    lin(R("ca", 3, 4), hcol, 32.0)
+    lin(R("ca", 5, 6), hcol, -32.0, 32.0)
+    lin(R("ca", 7, 8), ecol, 4.0)
+    lin(R("ca", 8, 9), p3, -1.0, -1.0)
+    lin(R("ca", 9, 10), lcol, -1.0)
+    lin(R("ca", 4, 5), acol, -96.0, R("ca", 9, 10))
+    for k in range(2):
+        act(R("et", 1024 * k, 1024 * k + 1024), R("idt", 0, 1024), AF.Copy, scale=0.0)
+    act(R("eye"), R("idt", 0, 128), AF.Identity, bias=0.5, scale=0.0)
+    iota("ir", [[1, 12], [0, 2]], 0, 0)
+    iota("ix", [[1, 4], [4, 10]], -4, 0)
+    iota("c4", [[1, 4]], 0, 0)
+    for k in range(2):
+        turn(R("tm", P * k, P * k + P), R("mk%d" % k, MO, MO + P))
+    tt(R("m1"), R("tm", 0, 2 * P, st=32), R("tm", 16, 2 * P, st=32), O.max)
+    ts(R("hv"), R("hv0"), lcol, None, O.add)
+    tt(R("mm"), R("m1", 0, 12), R("m1", 12, 24), O.max)
+    memset(R("zf", 0, 16), 0.0)
+    red(R("tot"), R("mm"), O.add)
+    scan(R("sn"), R("mm"))
+    ts(R("x0"), R("tri"), R("tot"), None, O.mult)
+    tt(R("g1"), R("sn"), R("dc1"), O.subtract)
+    turn(R("xt0"), R("x0"))
+    tt(R("g2"), R("g1"), R("mm"), O.mult)
+    red(R("base"), R("xt0"), O.add)
+    tt(R("g3"), R("g2"), R("dc"), O.add)
+    ts(R("cq", 3, 4), acol, float(r), float(-LC), O.is_gt, O.mult)
+    ts(R("wl"), R("g3"), R("base"), None, O.add)
+    ts(R("cq", 2, 3), acol, float(LC), R("cq", 3, 4), O.mult, O.add)
+    scatter(R("wn"), R("wl"), R("cv"))
+    ts(R("zp"), R("sn"), R("base"), R("cq", 2, 3), O.add, O.add)
+    turn(R("wnt"), R("wn", 0, LC))
+    memset(R("zz"), 0.0)
+    tt(R("zz", 0, 5), R("wnt", 0, LC, st=32), R("wnt", 16, LC, st=32), O.add)
+    ts(R("zp"), R("zp"), float(UR - 1), None, O.add)
+    turn(R("lr"), R("zz", 0, 32))
+    copy(R("zp", 0, 12, 32 * r, 32 * r + 32), R("plc", 0, 12, 32 * r, 32 * r + 32))
+    gather(R("ld"), R("lr"), R("hv"))
+    copy(R("rl"), R("ir"))
+    turn(R("ldt"), R("ld"))
+    copy(R("xl"), R("ix"))
+    for k in range(2):
+        copy(R("lst", k, 10, st=2), R("ldt", 32 * k, 32 * k + 5))
+    send([(q, R("lst"), R("lnd", 10 * here[q], 10 * here[q] + 10)) for q in others], "arl")
 
+    gather(R("zrep"), R("zp"), R("rl"), "s")
+    eye = R("eye")
+    op("p", lambda: g.affine_select(eye["ap"], eye["ap"], [[1, 128]], O.is_equal, 0.0, 0, -1), [eye], [eye])
+    for b in range(4):
+        copy(R("et", 513 * b, 512 * b + 512, st=4), eye, "s")
+    iota("ib", [[128, 4]], 0, 1)
+    iota("bo", [[8, 4]], 512, 0)
+    iota("cst0", [[32, 4]], 0, 0)
+    iota("c2b", [[32, 4], [16, 2]], 512, 0)
+    iota("c2a", [[4, 4], [0, 2]], 0, 0)
+    iota("cc0", [[-16, 6]], -P * r, 0)
+    iota("jc0", [[16, 24]], 0, 0)
     iota("t1", [[0, 128]], 0, 0)
-    iota("t2", [[0, 640]], 0, 0)
     quant("vq", 0, P, R("tbt"))
     for s in ("", "s"):
         dma("y", R("uc" + s, UB, UR), R("vq" + s), "du", 2)
         dma("y", R("mg" + s, 0, P), R("vq" + s), "dmg", 2)
-    memset(R("zf", 0, 16), 0.0)
     memset(R("zf", 400, 416), 0.0)
-    act(R("zf", 16, 400), pc, AF.Identity, bias=R("cq", 2, 3))
-    copy(R("zf", 16, 400, 32 * r, 32 * r + 32), R("idt", UB + 1, UB + 1 + P, 32 * r, 32 * r + 32), "s")
     for j in range(4):
         copy(R("cdp", 8 * j, 8 * j + 8), R("cdi", j, 32, st=4))
-    ts(R("g1"), R("cdp"), R("cq", 1, 2), 15.0, O.add, O.max)
+    ts(R("xl", 0, 40, st=10), R("c4"), R("ca", 7, 8), None, O.add)
+    ts(R("gx", 0, 32), R("cdp"), R("cq", 1, 2), 15.0, O.add, O.max)
+    turn(R("zf", 16, 400), R("zrep"))
+    tt(R("gx", 32, 64, st=2), R("gx", 1, 32, st=2), R("gx", 0, 32, st=2), O.subtract)
+    tt(R("gx", 33, 64, st=2), R("gx", 0, 32, st=2), R("gx", 1, 32, st=2), O.subtract)
     ts(R("pl", 0, 1), bcol, 8.0, gcol, O.mult, O.add)
-    ts(R("og", 0, 64, st=2), R("g1"), 400.0, None, O.min)
-    ts(R("og", 1, 64, st=2), R("g1"), 400.0, None, O.min)
-    gather(R("zr"), R("zf"), R("og"), "s")
+    ts(R("gx", 64, 96), R("gx", 32, 64), hcol, None, O.mult)
     gather(R("nc"), R("cdp"), R("pl", 0, 1))
-    copy(R("bl"), R("ib"))
-    copy(R("xl"), R("ix"))
-    ts(R("n1"), R("nc", 0, 8), 1.0, None, O.add)
-    ts(R("iw"), R("iv"), R("ca", 0, 1), None, O.add)
-    ts(R("dh"), R("im"), lcol, None, O.is_equal)
-    copy(R("nl"), R("n1", 0, 8, st=2))
-    ts(R("c2e"), R("c2a"), R("ca", 1, 2), None, O.add)
-    ts(R("c2f"), R("c2b"), lcol, None, O.add)
-    gather(R("nr"), R("idt"), R("nl"))
-    tt(R("dg"), R("dh"), R("iw"), O.mult)
-    ts(R("mj"), R("mj0"), p3, None, O.is_equal)
+    tt(R("gx", 96, 128), R("gx", 64, 96), R("gx", 0, 32), O.add)
+    ts(R("n1", 0, 8), R("nc", 0, 8), 1.0, None, O.add)
+    ts(R("og"), R("gx", 96, 128), 400.0, None, O.min)
 
     note(None, [R("lnd", 0, 30)], [], "arl", count["arl"])
     for a in range(4):
         copy(R("ls", 0, 30, 32 * a, 32 * a + 32), R("lnd", 0, 30, 32 * r, 32 * r + 32))
-    pick("pk", 0, 3 * LC, "vq", P, R("ls", 0, 30))
-    for s, k in (("", 0), ("s", 3)):
-        send([R("pk" + s, LC * k_, LC * k_ + LC) for k_ in range(3)], [R("uc" + s, UR + LC * here[q], UR + LC * here[q] + LC) for q in others], "arc", k)
+    for k, q in enumerate(others):
+        pick("pk", LC * k, LC * k + LC, "vq", P, R("ls", 10 * k, 10 * k + 10))
+        send([(q, R("pk", LC * k, LC * k + LC), R("uc", UR + LC * here[q], UR + LC * here[q] + LC))], "arc")
+    send([(q, R("pks", LC * k, LC * k + LC), R("ucs", UR + LC * here[q], UR + LC * here[q] + LC)) for k, q in enumerate(others)], "arc", 3)
 
-    iota("rp", [[0, 32]], 0, 0)
-    iota("kpr", [[0, 32]], 0, 0)
+    iota("t2", [[0, 256]], 0, 0, 0, 256)
     for k, q in enumerate([r] + others):
-        iota("keyi", [[4, 8], [1, 4], [0, 4]], 32 * q, 0, 128 * k, 128 * k + 128)
-    for k in range(2):
-        act(R("et", 1024 * k, 1024 * k + 1024), R("idt", 0, 1024), AF.Identity, bias=0.5, scale=0.0)
-    et = R("et")
-    op("p", lambda: g.affine_select(et["ap"], et["ap"], [[1, 4], [-1, 512]], O.is_equal, 0.0, 0, 4), [et], [et])
+        iota("keyi", [[8, 4], [1, 4], [0, 4]], 32 * q, 0, 64 * k, 64 * k + 64)
+    gather(R("zr"), R("zf"), R("og"), "s")
+    lin(R("cst"), R("cst0"), 1.0, R("ca", 0, 1))
+    lin(R("c2e"), R("c2a"), 1.0, R("ca", 0, 1))
+    lin(R("c2f"), R("c2b"), 1.0, lcol)
+    lin(R("n1", 8, 16), R("n1", 0, 8), 1.0 / 8192)
+    lin(R("cc"), R("cc0"), 1.0, R("ca", 4, 5))
+    lin(R("jc"), R("jc0"), 1.0, lcol)
+    lin(R("key"), R("keyi"), 1.0 / 256, R("ca", 1, 2))
 
+    copy(R("nl"), R("n1", 0, 8, st=2))
+    copy(R("bl", 0, 4), R("ib"))
+    ts(R("bl", 4, 8), R("bo"), gcol, None, O.add)
+    for j in range(3):
+        pick("ex", EX * j + 128, EX * j + EX, "xq", 128, R("xl", 10 * j, 10 * j + 9))
     turn(R("zt"), R("zr"))
-    tt(R("z1", 0, 32, 0, 64), R("zt", 0, 1024, 0, 64, 32), R("zt", 0, 1024, 64, 128, 32), O.add)
+    gather(R("nr"), R("idt"), R("nl"))
+    ev, od = R("z2", 0, 32, 0, 32, 2), R("z2", 1, 32, 0, 32, 2)
+    tt(R("z1", 0, 32, 0, 64), R("zt", 0, 512, 0, 64, 16), R("zt", 0, 512, 64, 128, 16), O.add)
     tt(R("z2", 0, 32, 0, 32), R("z1", 0, 32, 0, 32), R("z1", 0, 32, 32, 64), O.add)
+    tt(R("z2", 32, 48, 0, 32), od, ev, O.subtract)
+    ts(R("mk4"), R("c4"), p3, None, O.is_equal)
+    ts(R("z2", 48, 64, 0, 32), R("z2", 32, 48, 0, 32), R("pf", 1, 2, 0, 32), None, O.mult)
+    memset(R("al", 0, 1), 1.0)
+    tt(R("z2", 64, 96, 0, 32, 2), ev, R("z2", 48, 64, 0, 32), O.add)
+    tt(R("z2", 65, 96, 0, 32, 2), od, R("z2", 48, 64, 0, 32), O.subtract)
+    pick("ex", EX * 3 + 128, EX * 3 + EX, "xq", 128, R("xl", 30, 39))
     for a in range(4):
-        copy(R("sf", 0, 32, 32 * a, 32 * a + 32), R("z2", 0, 32, 0, 32))
-    for j in range(4):
-        pick("ex", 256 * j + 128, 256 * j + 256, "xq", 128, R("xl", 8 * j, 8 * j + 8))
-        if j == 0:
-            copy(R("sw"), R("sf"))
-            gather(R("sc"), R("sf"), R("pl", 0, 1))
-    for j in range(4):
-        ts(R("tie0", 16 * j, 16 * j + 16), R("nr", 16 * j, 16 * j + 16), R("nc", 2 * j, 2 * j + 1), None, O.is_lt)
+        copy(R("sf", 0, 32, 32 * a, 32 * a + 32), R("z2", 64, 96, 0, 32))
     tt(R("c2d"), R("c2e"), R("c2f"), O.subtract)
-    tt(R("tie"), R("tie0"), R("dg"), O.add)
+    copy(R("sw"), R("sf"))
+    gather(R("sc"), R("sf"), R("pl", 0, 1))
+    for j in range(4):
+        ts(R("tie", 16 * j, 16 * j + 16), R("nr", 16 * j, 16 * j + 16), R("nc", 2 * j, 2 * j + 1), -2.0 ** -100, O.is_lt, O.mult)
     ts(R("c2g", 0, 8, st=2), R("c2d", 0, 8, st=2), R("ca", 2, 3), None, O.mult)
     ts(R("c2g", 1, 8, st=2), R("c2d", 1, 8, st=2), hcol, None, O.mult)
-    ts(R("cc", 0, 3), R("cd0", 0, 3), R("ca", 4, 5), None, O.add)
+    ts(R("n1", 16, 24), R("sc", 0, 8), 1.0 / 8192, None, O.mult)
     tt(R("c2"), R("c2g"), R("c2f"), O.add)
-    ts(R("jc"), R("jc0"), lcol, None, O.add)
+    quant("wq", 0, 128, R("wt"))
 
     note(None, [R(n, UR, UW) for n in ("uc", "ucs")], [], "arc", count["arc"])
     for j in range(4):
-        pick("ex", 256 * j, 256 * j + 128, "uc", UW, R("sw", 8 * j, 8 * j + 8))
+        pick("ex", EX * j, EX * j + 128, "uc", UW, R("sw", 8 * j, 8 * j + 8))
     for j in range(4):
-        mm(BANKS[4 + j], 128, "ex", 256 * j + 128, "ex", 256 * j, 256 * j + 128)
-        mm(BANKS[j], 256, "ex", 256 * j, "ex", 256 * j, 256 * j + 256)
+        mm(BANKS[4 + j], 128, "ex", EX * j + 144, "ex", EX * j, EX * j + 128)
+        mm(BANKS[j], 136, "ex", EX * j, "ex", EX * j, EX * j + 136)
     for j in range(4):
-        copy(R("cs", 128 * j, 128 * j + 128), R(BANKS[4 + j], 0, 128), "s")
-        copy(R("cs", 512 + 128 * j, 640 + 128 * j), R(BANKS[j], 128, 256))
-    for j in range(4):
+        copy(R("cs", 128 * j, 128 * j + 128), R(BANKS[4 + j], 0, 128))
+        copy(R("cs", 512 + 8 * j, 520 + 8 * j), R(BANKS[j], 128, 136), "ssvv"[j])
         copy(R("cg", 128 * j, 128 * j + 128), R(BANKS[j], 0, 128), "s")
-    act(R("key"), R("keyi"), AF.Copy, scale=1.0 / 256)
     gather(R("ss"), R("cs"), R("bl"))
-    sr, so = R("ss", 0, 64), R("ss", 64, 128)
-    tt(R("a2"), sr, so, O.is_equal)
-    tt(R("w2", 0, 128, st=2), sr, so, O.is_gt)
-    tt(R("w2", 1, 128, st=2), R("a2"), R("tie"), O.mult)
+    row, own = R("ss", 0, 64), R("ss", 64, 128)
+    tt(R("dw"), row, own, O.subtract)
     gather(R("gg"), R("cg"), R("bl", 0, 4))
+    tt(R("w2"), R("dw"), R("tie"), O.is_gt)
+    tt(R("bb"), R("gg"), own, O.is_lt)
     for j in range(4):
-        red(R("rk", j, j + 1), R("w2", 32 * j, 32 * j + 32), O.add)
-    tt(R("bb"), R("gg"), so, O.is_ge)
-    copy(R("l1"), R("rk"))
-    ts(R("l2a", 0, 8, st=2), R("rk"), R("ca", 5, 6), None, O.mult)
-    ts(R("l2a", 1, 8, st=2), R("rk"), R("ca", 3, 4), None, O.mult)
-    scatter(R("t1"), R("l1"), R("bb"))
+        red(R("rk", j, j + 1), R("w2", 16 * j, 16 * j + 16), O.add)
+    tt(R("rk", 4, 8), R("rk", 0, 4), R("cst"), O.add)
+    ts(R("l2a", 0, 8, st=2), R("rk", 0, 4), R("ca", 5, 6), None, O.mult)
+    ts(R("l2a", 1, 8, st=2), R("rk", 0, 4), R("ca", 3, 4), None, O.mult)
+    copy(R("l1"), R("rk", 4, 8))
     tt(R("l2b"), R("l2a"), R("c2"), O.add)
-    copy(R("t1", 15, 128, st=16), R("n1"))
-    copy(R("t1", 14, 128, st=16), R("sc", 0, 8))
+    scatter(R("t1"), R("l1"), R("bb"))
     copy(R("l2"), R("l2b"))
+    copy(R("t1", 15, 128, st=16), R("n1", 8, 16))
+    copy(R("t1", 14, 128, st=16), R("n1", 16, 24))
     turn(R("t1t"), R("t1"))
     scatter(R("t2"), R("l2"), R("t1t"))
+    for k in range(1, 4):
+        copy(R("t2", k, 256, st=4), R("t2", 0, 256, st=4))
     turn(R("t2t"), R("t2", 0, 256))
-    tt(R("ff"), R("t2t", 0, 240), R("t2t", 16, 256), O.add)
-    for k in range(4):
-        copy(R("nn4", 8 * k, 8 * k + 8), R("ff", 15, 240, st=32), "s")
-    for k in range(4):
-        copy(R("sl4", 8 * k, 8 * k + 8), R("ff", 14, 240, st=32), "s")
-    memset(R("k8", 0, 1), 1.0)
+
+    def both(o, v, k):
+        tt(o, R("t2t", 32 * v + k, 256, st=32), R("t2t", 32 * v + 16 + k, 256, st=32), O.add)
+    both(R("al", 1, 8), 1, 0)
+    both(R("cu", 8, 14), 2, 1)
     for u in range(1, 7):
-        t, d = R("tmp", 8 * u, 8 * u + 7 - u), R("ff", 32 * (u + 1), 240, st=32)
-        ts(t, R("ff", 32 * (u + 1) + u, 240, st=32), R("ff", 32 * u, 32 * u + 1), None, O.is_gt)
-        tt(d, d, t, O.max)
-    ts(R("k8", 1, 8), R("ff", 32, 240, st=32), -1.0, 1.0, O.mult, O.add)
-    scan(R("cn"), R("k8"))
-    tt(R("ck"), R("cn"), R("k8"), O.mult)
-    for k in range(4):
-        ts(R("ck4", 8 * k, 8 * k + 8), R("ck"), float(k + 1), None, O.is_equal)
-
-    def rows(k, src):
-        tt(R("knm", 32 * k, 32 * k + 32), R("ck4"), R(src), O.mult)
-        for m in range(4):
-            red(R("kn", 4 * k + m, 4 * k + m + 1), R("knm", 32 * k + 8 * m, 32 * k + 8 * m + 8), O.add)
-        for m in range(4):
-            ts(R("lx", 32 * k + m, 32 * k + 32, st=4), R("mj"), R("kn", 4 * k + m, 4 * k + m + 1), None, O.mult)
-        turn(R("lxt", 32 * k, 32 * k + 32), R("lx", 32 * k, 32 * k + 32))
-        for h in range(2):
-            red(R("nl2", 2 * k + h, 2 * k + h + 1), R("lxt", 32 * k + 4 * h, 32 * k + 4 * h + 4), O.add)
-
-    def spread(o, c0, w, i, i0):
-        for a in range(4):
-            for b in range(4):
-                copy(R(o, c0 + w * a, c0 + w * a + w, 32 * b, 32 * b + 32), R(i, i0, i0 + w, 32 * a, 32 * a + 32), "vs"[b % 2])
-    rows(0, "nn4")
-    spread("nlf", 0, 2, "nl2", 0)
-    copy(R("kl"), R("nlf", 0, 8))
-    send([R("kl")] * 3, [R("kla", 8 * here[q], 8 * here[q] + 8) for q in others], "ark", 0)
+        w = 7 - u
+        ts(R("tmp", 8 * u, 8 * u + w), R("cu", 8 * u, 8 * u + w), R("al", u, u + 1), None, O.is_ge)
+        if u < 6:
+            both(R("cu", 8 * u + 8, 8 * u + 14 - u), u + 2, u + 1)
+        else:
+            both(R("sl8"), 0, 14)
+        tt(R("al", u + 1, 8), R("al", u + 1, 8), R("tmp", 8 * u, 8 * u + w), O.min)
+        if u == 1:
+            both(R("nn"), 0, 15)
+        if u == 2:
+            ts(R("mk8"), R("nn"), R("ca", 8, 9), None, O.add)
+    scan(R("cn"), R("al"))
+    tt(R("ck"), R("cn"), R("al"), O.mult)
+    tt(R("z8"), R("ck"), R("mk8"), O.add)
+    red(R("nlv"), R("z8"), O.min, True)
+    ts(R("nls"), R("nlv"), 8192.0, 1551.0, O.mult, O.min)
+    spread("kl", 1, "nls", 0, 1, qs="vsvsvsvsvsvsvsvv")
+    send([(q, R("kl"), R("kla", 4 * here[q], 4 * here[q] + 4)) for q in others], "ark")
 
     def rowsum(o, off, k):
         op("v", lambda: g.vector.tensor_tensor(o["ap"], R("idt")["ap"].indirect(off["ap"]), k["ap"], O.add), [o], [R("idt"), off, k])
-    rowsum(R("vr", 0, 128), R("kl"), R("key", 0, 128))
-    for k in range(3):
-        act(R("abo", 128 * k, 128 * k + 128), R("vr", 0, 128), AF.Abs, bias=R("cc", k, k + 1))
+    ts(R("ms8"), R("sl8"), R("ca", 8, 9), None, O.add)
+    rowsum(R("vr", 0, 64), R("kl"), R("key", 0, 64))
+    for k in range(6):
+        act(R("abo", 64 * k, 64 * k + 64), R("vr", 0, 64), AF.Abs, bias=R("cc", k, k + 1))
     quant("eq", 0, 512, R("et"))
-    quant("wq", 0, 128, R("wt"))
-    ts(R("kpr", 0, 4), R("kn", 0, 4), -1.0, None, O.add)
     for ch in range(2):
         for b in range(4):
             mm(BANKS[4 * ch + b], 192, "eq", 128 * b, "vq", 192 * ch, 192 * ch + 192, True, False)
-    turn(R("kpt"), R("kpr"))
-    for a in range(4):
-        dma("y", T.kp[:, 8 * a:8 * a + 8], R("kpt", 0, 8, 32 * a, 32 * a + 4), "dk", 4)
-    for k in range(3):
-        red(R("ab", 392 * k + 384, 392 * k + 385), R("abo", 128 * k, 128 * k + 128), O.min)
+    tt(R("y8"), R("ck"), R("ms8"), O.add)
+    ts(R("kt"), R("nlv"), 0.5, 8192.0, O.is_lt, O.mult)
+    red(R("slv"), R("y8"), O.min, True)
+    tt(R("kv"), R("nlv"), R("kt"), O.mult)
+    ts(R("yv"), R("slv"), 0.5, 8192.0, O.is_lt, O.mult)
+    ts(R("zz", 64, 68), R("mk4"), R("kv"), None, O.mult)
+    tt(R("zz", 96, 97), R("slv"), R("yv"), O.mult)
+    for k in range(2):
+        red(R("ab", 200 * k + 192, 200 * k + 193), R("abo", 64 * k, 64 * k + 64), O.min)
+    turn(R("yr"), R("zz", 96, 128))
+    red(R("ab", 592, 593), R("abo", 128, 192), O.min)
+    gather(R("yd"), R("yr"), R("hv"))
+    red(R("ab", 792, 793), R("abo", 192, 256), O.min)
+    turn(R("ydt"), R("yd"))
+    for k in range(4, 6):
+        red(R("ab", 200 * k + 192, 200 * k + 193), R("abo", 64 * k, 64 * k + 64), O.min)
 
     note(None, [R("kla")], [], "ark", count["ark"])
-    for s in (0, 192):
-        rowsum(R("vr", 128 + s, 320 + s), R("kla", s // 16, s // 16 + 12), R("key", 128 + s, 320 + s))
-        for k in range(3):
-            act(R("ab", 392 * k + s, 392 * k + s + 192), R("vr", 128 + s, 320 + s), AF.Abs, bias=R("cc", k, k + 1))
-    for k in range(3):
-        red(R("rp", k, k + 1), R("ab", 392 * k, 392 * k + 385), O.min)
-    turn(R("rpt"), R("rp"))
-    for c in range(4):
-        s = 16 * (c // 2)
-        copy(R("rd", 16 * c, 16 * c + 16), R("rpt", s, s + 16), "vs"[c % 2])
-    turn(R("rdt"), R("rd"))
-    copy(R("lc", 0, 6, st=2), R("rdt", 0, 3))
-    copy(R("lc", 1, 6, st=2), R("rdt", 32, 35))
-    spread("lnf", 0, 6, "lc", 0)
-    ts(R("ln"), R("lnf"), 256.0, 127.0, O.mult, O.min)
+    vo = R("vr", 64, 256)
+    rowsum(vo, R("kla"), R("key", 64, 256))
+    for k in range(4):
+        act(R("ab", 200 * k, 200 * k + 192), vo, AF.Abs, bias=R("cc", k, k + 1))
+    spread("ksl", 2, "ydt", 0, 64, 32, 0, 3, "s")
+    for k in (4, 5):
+        ts(R("ab", 200 * k, 200 * k + 192), vo, R("cc", k, k + 1), None, O.add)
+    for k in (4, 5, 0, 1, 2, 3):
+        red(R("zz", 32 + k, 33 + k), R("ab", 200 * k, 200 * k + 193), O.min, True)
+    turn(R("kpt"), R("zz", 64, 96))
+    turn(R("rpt"), R("zz", 32, 64))
+    tt(R("kp2"), R("kpt", 0, 32, st=2), R("kpt", 1, 32, st=2), O.add)
+    for k in range(2):
+        tt(R("dmn", 16 * k, 16 * k + 16), R("rpt", 0, 16), R("rpt", 16, 32), O.min)
+    tt(R("kp3"), R("kp2", 0, 16, st=2), R("kp2", 1, 16, st=2), O.add)
+    turn(R("lc"), R("dmn"))
+    ts(R("kpo"), R("kp3"), -1.0, None, O.add)
+    ts(R("lcs"), R("lc", 0, 6), 256.0, 128.0, O.mult, O.min)
+    for a in range(4):
+        dma("y", T.kp[:, 8 * a:8 * a + 8], R("kpo", 0, 8, 32 * a, 32 * a + 4), "dk", 4)
 
     note(None, [R("xa" + s, 32 * q, 32 * q + 32) for q in others for s in ("", "s")], [], "arx", count["arx"])
     for ch in range(2):
-        pick("qp", 192 * ch, 192 * ch + 192, "xa", 128, R("ln", 12 * ch, 12 * ch + 12))
+        spread("ln", 6, "lcs", 0, 6, lo=2 * ch, hi=2 * ch + 2, qs="vsvvsvsv")
+        pick("qp", 192 * ch, 192 * ch + 192, "xa", 160, R("ln", 12 * ch, 12 * ch + 12))
     for ch in range(2):
         for b in range(4):
             mm(BANKS[4 * ch + b], 192, "eq", 128 * b, "qp", 192 * ch, 192 * ch + 192, False, True)
-    ts(R("sl0"), R("lnf"), 0.5, 384.0, O.is_lt, O.mult)
-    rows(1, "sl4")
+    ts(R("sl0"), R("ln"), 127.5, 384.0, O.is_lt, O.mult)
+    spread("ksl", 2, "ydt", 0, 64, 32, 3, 4, "v")
     tt(R("sl1"), R("sl0"), R("jc"), O.add)
-    copy(R("sl"), R("sl1"))
-    for ch in range(2):
-        for b in range(4):
-            copy(R("nt", 768 * ch + b, 768 * ch + 768, st=4), R(BANKS[4 * ch + b], 0, 192), "vs"[b % 2])
+
+    def half(ch, bs):
+        for b in bs:
+            copy(R("nt", 768 * ch + b, 768 * ch + 768, st=4), R(BANKS[4 * ch + b], 0, 192), "sv"[b % 2])
+
+    def new(ch):
         quant("mg", P + 192 * ch, P + 192 * ch + 192, R("nt", 768 * ch, 768 * ch + 768))
-        if ch == 0:
-            spread("nlf", 8, 2, "nl2", 2)
-            copy(R("ksl"), R("nlf", 8, 16))
-            pick("kq", 0, 128, "uc", UW, R("ksl"))
-            mm(BANKS[0], 128, "wq", 0, "kq", 0, 128)
+
+    def store(ch, late):
         pick("oq", 192 * ch, 192 * ch + 192, "mg", 2 * P, R("sl", 12 * ch, 12 * ch + 12))
         dma("y", T.oc[:, 768 * ch:768 * ch + 768], R("oq", 192 * ch, 192 * ch + 192), "do%d" % ch, 1)
         for k in range(4):
-            dma("sy"[k % 2], T.osc[4 * k:4 * k + 4, 192 * ch:192 * ch + 192], R("oqs", 192 * ch, 192 * ch + 192, 32 * k, 32 * k + 4), "dp%d" % ch, 4)
-        if ch == 0:
-            copy(R("yt"), R(BANKS[0], 0, 128), "s")
-            dma("s", T.y[:, :], R("yt"), "dy", 1)
+            dma("sy"[k % 2] if late else "y", T.osc[4 * k:4 * k + 4, 192 * ch:192 * ch + 192], R("oqs", 192 * ch, 192 * ch + 192, 32 * k, 32 * k + 4), "dp%d" % ch, 4)
+    half(0, (0, 1, 2))
+    copy(R("sl"), R("sl1"))
+    pick("kq", 0, 128, "uc", UW, R("ksl"), "v")
+    half(0, (3,))
+    pick("kq", 0, 128, "uc", UW, R("ksl"), "s")
+    mm(BANKS[0], 128, "wq", 0, "kq", 0, 128)
+    new(0)
+    half(1, (0, 2))
+    store(0, False)
+    half(1, (1, 3))
+    copy(R("yt"), R(BANKS[0], 0, 128), "s")
+    dma("y", T.y[:, :], R("yt"), "dy", 1)
+    new(1)
+    store(1, True)
 
     for s in sorted(count):
         g.wait_ge(T.sem[s], count[s])

@@ -8,31 +8,34 @@ UW = UR + 3 * LC
 MO = 3 * P
 MW = MO + 4 * P
 DB = P
-EX = 272
+DUMP = N * P + 4
+IW = DUMP + 20
+CUT = ((0, 160), (160, 384))
 
 F32, BF, I32, U16, U8, F8 = "float32", "bfloat16", "int32", "uint16", "uint8", "float8_e4m3fn_x4"
 SCRATCH = {}
 for _d, _names in (
     (BF, "tbt:1536 xt:512 wt:512 et:2048 nt:1536"),
-    (F8, "vq:384 xq:128 wq:128 eq:512 xa:160 uc:896 pk:480 ex:1088 kq:128 qp:384 mg:768 oq:384"),
-    (U8, "vqs:384 xqs:128 wqs:128 eqs:512 xas:160 ucs:896 pks:480 exs:1088 kqs:128 qps:384 mgs:768 oqs:384"),
-    (I32, "kci:96"), (U16, "bl:8 xl:40 pl:2 rl:24 hv:4"), (BF, "ones:16 eye:128"),
-    (F32, "kcf:512 idt:1552 key:256 keyi:256 cv:192 zz:128"),
+    (F8, "vq:384 xq:128 wq:128 eq:512 xa:160 uc:896 pk:480 ex:512 kq:128 qp:384 mg:768 oq:384"),
+    (U8, "vqs:384 xqs:128 wqs:128 eqs:512 xas:160 ucs:896 pks:480 exs:512 kqs:128 qps:384 mgs:768 oqs:384"),
+    (I32, "kci:64"), (U16, "bl:4 bo:8 br:4 pl:2 rl:24 hv:4"), (BF, "ones:16 eye:128 ptv:64"),
+    (F32, "kcf:512 idt:1560 ids:1560 cv:192 zz:128"),
     (I32, "cdh:16 cdi:32"), (U16, "off:32 wl:12 lst:10 lnd:30 ls:30"), (BF, "mk0:2688 mk1:2688 tm:768 m1:24"),
     (F32, "req:192 x0:32 xt0:32 wn:1152 wnt:160 lr:32 ld:64 ldt:64"),
-    (F32, "cdp:32 zp:12 zrep:384 zf:416 gx:128 zr:512 zt:512 z1:32 z2:128 sf:32 sc:16 nc:16 n1:24 nr:64 tie:64"), (U16, "og:32 sw:32 nl:4"),
-    (F32, "cs:544 cg:512 ss:128 gg:64 dw:64 w2:64 bb:64 rk:8 l2a:8 l2b:8 t1:128 t1t:128 t2:640 t2t:256 cu:64 tmp:64"), (U16, "l1:4 l2:8"),
-    (F32, "pr:128 kpt:32 yr:32 yd:64 ydt:64 yt:128"), (U16, "kl:4 ksl:8 kla:12"),
-    (F32, "vr:256 abo:384 ab:1200 rpt:32 dmn:32 lc:32 lcs:6 sl0:24 sl1:24"), (U16, "ln:24 sl:24"),
+    (F32, "cdp:32 zp:12 zrep:384 zf:416 gx:128 zr:512 zt:512 z2:128 sf:32 sc:16 nc:16 n1:24 nr:64 tie:64"), (U16, "og:32 sw:32 nl:4 kl:2"),
+    (F32, "cs:128 cg:512 ob:128 obt:128 row:64 gg:64 dw:64 w2:64 bb:64 rks:68 l2a:8 l2b:8 t1:128 t1t:128 t2:640 t2t:256 cu:64 tmp:64 alg:64"), (U16, "l1:4 l2:8"),
+    (F32, "pr:160 kpt:32 yr:32 yd:64 ydt:64 yt:128"), (U16, "kd:2 ksl:8 kla:6"),
+    (BF, "wk:1568 wo:1568 tk:384 tko:384"), (F32, "wm:64 sl0:24 sl1:24"), (U16, "ln:24 sl:24"),
 ):
     for _n in _names.split():
         SCRATCH[_n.split(":")[0]] = ("sbuf", [128, int(_n.split(":")[1])], _d)
 PART = {}
 for _d, _names in (
-    ("kcf", "pf:8 cq:8 ca:12 t32:32 tri:32 dc0:12 dc:12 dc1:12 plc:12 c4:4 bo:4 hv0:4 c2a:8 c2b:8 c2e:8 c2f:8 c2d:8 c2g:8 c2:8 cst0:4 cst:4 cc0:6 cc:6 jc0:24 jc:24 mk4:4"),
-    ("kci", "ip:2 ib:4 ix:40 it:8 ir:24"),
+    ("kcf", "pf:8 cq:8 ca:12 t32:32 tri:32 dc0:12 dc:12 dc1:12 plc:12 c4:4 bo0:8 br0:4 br1:4 hv0:4 c2:8 cst0:4 cst:4 jc0:24 jc:24 mk4:4 rst0:64 rst:64 pm0:16 pm:16 pt0:64"),
+    ("kci", "ip:2 ib:4 it:8 ir:24"),
     ("req", "mm:12 tot:1 base:1 sn:12 g1:12 g2:12 g3:12"),
-    ("pr", "al:8 nn:8 sl8:8 mk8:8 ms8:8 cn:8 ck:8 z8:8 y8:8 nlv:1 nls:1 slv:1 kt:1 kv:1 yv:1 kp2:16 kp3:8 kpo:8"),
+    ("pr", "nn:8 sl8:8 mk8:8 ms8:8 ms9:8 cn:8 ck:8 z8:8 y8:8 nlv:1 nls:1 slv:1 kt:1 kw:1 kv:1 yv:1 kp2:16 kp3:8 kpo:8 own:16 same:16 dup:1"),
+    ("wm", "wa:12 wb:12 wc:12 wown:12"),
 ):
     _c = 0
     for _n in _names.split():
@@ -42,7 +45,7 @@ for _d, _names in (
 BANKS = ["pb%d" % _b for _b in range(8)]
 for _n in BANKS:
     SCRATCH[_n] = ("psum", [128, 512], F32)
-SEMAPHORES = ["ev", "ec", "et_", "ep", "dch", "dcd", "dx", "dtb", "dw", "du", "dxa", "dmg", "dz", "dk", "dy", "do0", "do1", "dp0", "dp1",
+SEMAPHORES = ["ev", "ec", "et_", "ep", "dch", "dcd", "dx", "dtb", "dw", "dxa", "dmg", "dz", "dk", "dy", "do0", "do1", "dp0", "dp1",
               "arx", "arl", "arc", "ark", "loc"]
 
 
@@ -125,6 +128,9 @@ def rank_program(g, core, T, topo):
     def tt(o, a, b, f):
         op("v", lambda: g.vector.tensor_tensor(o["ap"], a["ap"], b["ap"], f), [o], [a, b])
 
+    def ttg(o, win, off, b, f):
+        op("v", lambda: g.vector.tensor_tensor(o["ap"], win["ap"].indirect(off["ap"]), b["ap"], f), [o], [win, off, b])
+
     def ts(o, a, s1, s2, f1, f2=None):
         ins = [a] + [s for s in (s1, s2) if isinstance(s, dict)]
         v1 = s1["ap"] if isinstance(s1, dict) else s1
@@ -138,17 +144,13 @@ def rank_program(g, core, T, topo):
         kw = {"apply_absolute_value": True} if size else {}
         op("v", lambda: g.vector.tensor_reduce(o["ap"], a["ap"], X, f, **kw), [o], [a])
 
-    def scan(o, a):
-        op("v", lambda: g.vector.tensor_tensor_scan(o["ap"], a["ap"], a["ap"], 0.0, O.add, O.max), [o], [a])
+    def scan(o, a, b, f1, f2):
+        op("v", lambda: g.vector.tensor_tensor_scan(o["ap"], a["ap"], b["ap"], 0.0, f1, f2), [o], [a, b])
 
-    def act(o, a, f, bias=None, scale=1.0):
-        kw = {"scale": scale}
-        if bias is not None:
-            kw["bias"] = bias["ap"] if isinstance(bias, dict) else bias
-        op("s", lambda: g.scalar.activation(o["ap"], a["ap"], f, **kw), [o], [a] + ([bias] if isinstance(bias, dict) else []))
-
-    def lin(o, a, scale=1.0, bias=0.0):
-        act(o, a, AF.Identity, bias=bias, scale=scale)
+    def lin(o, a, scale=1.0, bias=0.0, f=AF.Identity):
+        ins = [a] + [s for s in (scale, bias) if isinstance(s, dict)]
+        kw = {"scale": scale["ap"] if isinstance(scale, dict) else scale, "bias": bias["ap"] if isinstance(bias, dict) else bias}
+        op("s", lambda: g.scalar.activation(o["ap"], a["ap"], f, **kw), [o], ins)
 
     def turn(o, a):
         op("v", lambda: g.vector.transpose(o["ap"], a["ap"]), [o], [a])
@@ -162,12 +164,10 @@ def rank_program(g, core, T, topo):
     def scatter(win, off, i):
         op("v", lambda: g.vector.tensor_copy(win["ap"].indirect(off["ap"]), i["ap"]), [win], [off, i])
 
-    def pick(cn, o0, o1, wn, w1, off, q="vs"):
+    def pick(cn, o0, o1, wn, w1, off):
         o, w = R(cn, o0, o1), R(wn, 0, w1)
-        if "v" in q:
-            op("v", lambda: g.vector.tensor_copy(o["ap"].bitcast(dt.uint32), w["ap"].bitcast(dt.uint32).indirect(off["ap"])), [o], [w, off])
-        if "s" in q:
-            gather(R(cn + "s", o0, o1), R(wn + "s", 0, w1), off, "s")
+        op("v", lambda: g.vector.tensor_copy(o["ap"].bitcast(dt.uint32), w["ap"].bitcast(dt.uint32).indirect(off["ap"])), [o], [w, off])
+        gather(R(cn + "s", o0, o1), R(wn + "s", 0, w1), off, "s")
 
     def quant(cn, c0, c1, tile):
         o, s = R(cn, c0, c1), R(cn + "s", c0, c1)
@@ -179,11 +179,10 @@ def rank_program(g, core, T, topo):
 
     def iota(name, pattern, base, cm, c0=0, c1=None):
         o = R(name, c0, c1)
-        kw = {"allow_small_or_imprecise_dtypes": True} if SCRATCH[o["n"]][2] == F32 else {}
+        kw = {"allow_small_or_imprecise_dtypes": True} if SCRATCH[o["n"]][2] in (F32, BF) else {}
         op("p", lambda: g.iota(o["ap"], pattern, base, cm, **kw), [o], [])
 
     others = [q for q in range(N) if q != r]
-    at = {q: k for k, q in enumerate(others)}
     here = {q: (r if r < q else r - 1) for q in others}
 
     def send(pieces, sem, turned=0):
@@ -201,35 +200,31 @@ def rank_program(g, core, T, topo):
             count[sem] = count.get(sem, 0) + m
         g.remote_dma_fused(tr, local_sem=T.sem.loc)
 
-    def spread(o, n, i, c0, n0, st=1, lo=0, hi=4, qs="vs"):
-        k = 0
-        for a in range(lo, hi):
-            for b in range(4):
-                copy(R(o, n * a, n * a + n, 32 * b, 32 * b + 32), R(i, c0, n0, 32 * a, 32 * a + 32, st), qs[k % len(qs)])
-                k += 1
-
     for k in range(8):
         dma("ys"[k % 2], R("cdh", 0, 16, 16 * k, 16 * k + 16), T.cd[:, 16 * (k % 2):16 * (k % 2) + 16], "dch", 8)
     dma("y", R("xt", 0, 128), T.x[:, :], "dx", 1)
-    dma("s", R("tbt"), T.tb[:, :], "dtb", 1)
+    dma("y", R("tbt"), T.tb[:, :], "dtb", 1)
     for k in range(8):
-        dma("ys"[k % 2], R("cdi", 0, 32, 16 * k, 16 * k + 16), T.cd[:, :], "dcd", 8)
+        dma("y", R("cdi", 0, 32, 16 * k, 16 * k + 16), T.cd[:, :], "dcd", 8)
     dma("y", R("wt"), T.w[:, :], "dw", 1)
 
+    IQ = IW // 4
     iota("ip", [[1, 1]], 0, 1, 0, 1)
     iota("t32", [[1, 32]], 0, 0)
     iota("dc0", [[1, 12]], DB, 0)
     iota("cv", [[32, 12], [1, 16]], 0, 0)
+    iota("idt", [[1, IQ]], 0, 0, 0, IQ)
     iota("hv0", [[16, 2], [0, 2]], 0, 0)
     iota("plc", [[32, 12]], UB - 32 * r, 1)
-    iota("idt", [[1, 1552]], -1, 0)
+    iota("ir", [[1, 12], [0, 2]], 0, 0)
+    iota("c4", [[1, 4]], 0, 0)
     memset(R("mk0", MO, MO + P), 0.0)
     p = R("ip", 0, 1)
     for k, (sh, msk) in enumerate(((0, 15), (4, 1), (0, 7), (4, 7), (0, 3), (5, 3), (0, 31), (1, 3))):
         ts(R("it", k, k + 1), p, sh, msk, O.logical_shift_right, O.bitwise_and)
     memset(R("mk1", MO, MO + P), 0.0)
     copy(R("pf", 0, 8), R("it", 0, 8))
-    lcol, hcol, ecol, gcol, p3, acol, pcol, bcol = [R("pf", k, k + 1) for k in range(8)]
+    lcol, hcol, _ecol, gcol, p3, acol, pcol, bcol = [R("pf", k, k + 1) for k in range(8)]
     memset(R("ones"), 1.0)
     ts(R("cq", 0, 1), acol, float(-P), float(MO), O.mult, O.add)
     memset(R("xt", 128, 512), 0.0)
@@ -242,42 +237,42 @@ def rank_program(g, core, T, topo):
     memset(R("wn", 0, LC), 0.0)
     ts(R("off", 0, 32, st=2), R("cdh"), R("cq", 0, 1), None, O.add)
 
-    def points():
-        quant("xq", 0, 128, R("xt"))
-        for s, k in (("", 0), ("s", 3)):
-            send([(q, R("xq" + s, 0, 32), R("xa" + s, 32 * r, 32 * r + 32)) for q in others], "arx", k)
-        for s in ("", "s"):
-            dma("y", R("uc" + s, 0, 32), R("xq" + s, 32, 64), "dz", 2)
-            dma("y", R("xa" + s, 32 * r, 32 * r + 32), R("xq" + s, 0, 32), "dxa", 4)
-            dma("y", R("xa" + s, 128, 160), R("xq" + s, 32, 64), "dxa", 4)
-
     for i in range(A // 2):
         scatter(R("mk%d" % (i % 2)), R("off", 2 * i, 2 * i + 1), R("ones"))
-        if i == 3:
-            points()
+    for k in range(2):
+        turn(R("tm", P * k, P * k + P), R("mk%d" % k, MO, MO + P))
+
+    quant("xq", 0, 128, R("xt"))
+    for s, k in (("", 0), ("s", 3)):
+        send([(q, R("xq" + s, 0, 32), R("xa" + s, 32 * r, 32 * r + 32)) for q in others], "arx", k)
+    for s in ("", "s"):
+        dma("y", R("uc" + s, 0, 32), R("xq" + s, 32, 64), "dz", 2)
+        dma("y", R("xa" + s, 32 * r, 32 * r + 32), R("xq" + s, 0, 32), "dxa", 4)
+        dma("y", R("xa" + s, 128, 160), R("xq" + s, 32, 64), "dxa", 4)
+
     lin(R("cq", 1, 2), acol, float(-P), 16.0)
-    lin(R("ca", 1, 2), hcol, 4.0 / 256)
+    lin(R("ca", 1, 2), gcol, 4.0)
+    lin(R("ca", 4, 5), lcol, 1.0, float(DUMP))
     lin(R("ca", 2, 3), hcol, -1.0, 1.0)
     lin(R("ca", 3, 4), hcol, 32.0)
     lin(R("ca", 5, 6), hcol, -32.0, 32.0)
-    lin(R("ca", 7, 8), ecol, 4.0)
     lin(R("ca", 8, 9), p3, -1.0, -1.0)
-    lin(R("ca", 9, 10), lcol, -1.0)
-    lin(R("ca", 4, 5), acol, -96.0, R("ca", 9, 10))
-    for k in range(2):
-        act(R("et", 1024 * k, 1024 * k + 1024), R("idt", 0, 1024), AF.Copy, scale=0.0)
-    act(R("eye"), R("idt", 0, 128), AF.Identity, bias=0.5, scale=0.0)
-    iota("ir", [[1, 12], [0, 2]], 0, 0)
-    iota("ix", [[1, 4], [4, 10]], -4, 0)
-    iota("c4", [[1, 4]], 0, 0)
-    for k in range(2):
-        turn(R("tm", P * k, P * k + P), R("mk%d" % k, MO, MO + P))
+    for k in range(8):
+        lin(R("et", 256 * k, 256 * k + 256), R("idt", 0, 256), 0.0)
+    eye, nil = R("eye"), R("et", 0, 128)
+    op("p", lambda: g.affine_select(eye["ap"], nil["ap"], [[1, 128]], O.not_equal, 0.5, 0, -1), [eye], [nil])
+    for k in range(1, 4):
+        lin(R("idt", IQ * k, IQ * k + IQ), R("idt", 0, IQ), 1.0, float(IQ * k))
+    for j in range(4):
+        copy(R("cdp", 8 * j, 8 * j + 8), R("cdi", j, 32, st=4), "s")
+    for b in range(4):
+        copy(R("et", 513 * b, 512 * b + 512, st=4), eye, "s")
     tt(R("m1"), R("tm", 0, 2 * P, st=32), R("tm", 16, 2 * P, st=32), O.max)
     ts(R("hv"), R("hv0"), lcol, None, O.add)
     tt(R("mm"), R("m1", 0, 12), R("m1", 12, 24), O.max)
     memset(R("zf", 0, 16), 0.0)
     red(R("tot"), R("mm"), O.add)
-    scan(R("sn"), R("mm"))
+    scan(R("sn"), R("mm"), R("mm"), O.add, O.max)
     ts(R("x0"), R("tri"), R("tot"), None, O.mult)
     tt(R("g1"), R("sn"), R("dc1"), O.subtract)
     turn(R("xt0"), R("x0"))
@@ -298,32 +293,22 @@ def rank_program(g, core, T, topo):
     gather(R("ld"), R("lr"), R("hv"))
     copy(R("rl"), R("ir"))
     turn(R("ldt"), R("ld"))
-    copy(R("xl"), R("ix"))
     for k in range(2):
-        copy(R("lst", k, 10, st=2), R("ldt", 32 * k, 32 * k + 5))
+        copy(R("lst", k, 10, st=2), R("ldt", 32 * k, 32 * k + 5), "vs"[k])
     send([(q, R("lst"), R("lnd", 10 * here[q], 10 * here[q] + 10)) for q in others], "arl")
 
     gather(R("zrep"), R("zp"), R("rl"), "s")
-    eye = R("eye")
-    op("p", lambda: g.affine_select(eye["ap"], eye["ap"], [[1, 128]], O.is_equal, 0.0, 0, -1), [eye], [eye])
-    for b in range(4):
-        copy(R("et", 513 * b, 512 * b + 512, st=4), eye, "s")
+    iota("br0", [[32, 4]], 0, 0)
+    iota("rst0", [[0, 4], [1, 16]], 0, 0)
+    iota("pm0", [[4, 4], [0, 4]], 3, 0)
     iota("ib", [[128, 4]], 0, 1)
-    iota("bo", [[8, 4]], 512, 0)
+    iota("bo0", [[33, 4], [0, 2]], 0, 0)
     iota("cst0", [[32, 4]], 0, 0)
-    iota("c2b", [[32, 4], [16, 2]], 512, 0)
-    iota("c2a", [[4, 4], [0, 2]], 0, 0)
-    iota("cc0", [[-16, 6]], -P * r, 0)
+    iota("pt0", [[A, N], [1, 4], [0, 4]], 0, 0)
     iota("jc0", [[16, 24]], 0, 0)
-    iota("t1", [[0, 128]], 0, 0)
     quant("vq", 0, P, R("tbt"))
-    for s in ("", "s"):
-        dma("y", R("uc" + s, UB, UR), R("vq" + s), "du", 2)
-        dma("y", R("mg" + s, 0, P), R("vq" + s), "dmg", 2)
     memset(R("zf", 400, 416), 0.0)
-    for j in range(4):
-        copy(R("cdp", 8 * j, 8 * j + 8), R("cdi", j, 32, st=4))
-    ts(R("xl", 0, 40, st=10), R("c4"), R("ca", 7, 8), None, O.add)
+    quant("uc", UB, UR, R("tbt"))
     ts(R("gx", 0, 32), R("cdp"), R("cq", 1, 2), 15.0, O.add, O.max)
     turn(R("zf", 16, 400), R("zrep"))
     tt(R("gx", 32, 64, st=2), R("gx", 1, 32, st=2), R("gx", 0, 32, st=2), O.subtract)
@@ -332,193 +317,204 @@ def rank_program(g, core, T, topo):
     ts(R("gx", 64, 96), R("gx", 32, 64), hcol, None, O.mult)
     gather(R("nc"), R("cdp"), R("pl", 0, 1))
     tt(R("gx", 96, 128), R("gx", 64, 96), R("gx", 0, 32), O.add)
-    ts(R("n1", 0, 8), R("nc", 0, 8), 1.0, None, O.add)
     ts(R("og"), R("gx", 96, 128), 400.0, None, O.min)
 
     note(None, [R("lnd", 0, 30)], [], "arl", count["arl"])
     for a in range(4):
-        copy(R("ls", 0, 30, 32 * a, 32 * a + 32), R("lnd", 0, 30, 32 * r, 32 * r + 32))
+        copy(R("ls", 0, 30, 32 * a, 32 * a + 32), R("lnd", 0, 30, 32 * r, 32 * r + 32), "vs"[a % 2])
     for k, q in enumerate(others):
         pick("pk", LC * k, LC * k + LC, "vq", P, R("ls", 10 * k, 10 * k + 10))
         send([(q, R("pk", LC * k, LC * k + LC), R("uc", UR + LC * here[q], UR + LC * here[q] + LC))], "arc")
     send([(q, R("pks", LC * k, LC * k + LC), R("ucs", UR + LC * here[q], UR + LC * here[q] + LC)) for k, q in enumerate(others)], "arc", 3)
 
+    iota("t1", [[0, 128]], 0, 0)
     iota("t2", [[0, 256]], 0, 0, 0, 256)
-    for k, q in enumerate([r] + others):
-        iota("keyi", [[8, 4], [1, 4], [0, 4]], 32 * q, 0, 64 * k, 64 * k + 64)
+    for n in ("wk", "wo"):
+        iota(n, [[0, P]], N * A, 0, P * r, P * r + P)
+    lin(R("br1"), R("br0"), 1.0, R("ca", 0, 1))
+    for j in range(4):
+        lin(R("gg", 16 * j, 16 * j + 16), R("t32", 0, 16), 0.0, R("nc", 2 * j, 2 * j + 1))
     gather(R("zr"), R("zf"), R("og"), "s")
     lin(R("cst"), R("cst0"), 1.0, R("ca", 0, 1))
-    lin(R("c2e"), R("c2a"), 1.0, R("ca", 0, 1))
-    lin(R("c2f"), R("c2b"), 1.0, lcol)
-    lin(R("n1", 8, 16), R("n1", 0, 8), 1.0 / 8192)
-    lin(R("cc"), R("cc0"), 1.0, R("ca", 4, 5))
+    lin(R("n1", 8, 16), R("nc", 0, 8), 1.0 / 8192)
     lin(R("jc"), R("jc0"), 1.0, lcol)
-    lin(R("key"), R("keyi"), 1.0 / 256, R("ca", 1, 2))
+    lin(R("ptv"), R("pt0"), 1.0, R("ca", 1, 2))
+    lin(R("ca", 7, 8), hcol, 28.0, 4.0)
+    lin(R("ca", 9, 10), hcol, -28.0, 32.0)
+    lin(R("ca", 10, 11), hcol, 512.0)
+    lin(R("ca", 11, 12), hcol, -512.0, 528.0)
+    lin(R("cq", 4, 5), lcol, hcol, R("ca", 10, 11))
+    lin(R("cq", 5, 6), lcol, R("ca", 2, 3), R("ca", 11, 12))
+    lin(R("c2", 0, 8, st=2), R("c4"), R("ca", 7, 8), R("cq", 4, 5))
+    lin(R("c2", 1, 8, st=2), R("c4"), R("ca", 9, 10), R("cq", 5, 6))
 
-    copy(R("nl"), R("n1", 0, 8, st=2))
-    copy(R("bl", 0, 4), R("ib"))
-    ts(R("bl", 4, 8), R("bo"), gcol, None, O.add)
-    for j in range(3):
-        pick("ex", EX * j + 128, EX * j + EX, "xq", 128, R("xl", 10 * j, 10 * j + 9))
+    copy(R("nl"), R("nc", 0, 8, st=2))
+    ts(R("br"), R("br1"), lcol, None, O.add)
+    ts(R("rst"), R("rst0"), 0.5, None, O.is_gt)
+    ts(R("pm"), R("pm0"), lcol, 4096.0, O.is_ge, O.mult)
+    memset(R("kd"), 0.0)
+    quant("wq", 0, 128, R("wt"))
+    quant("eq", 0, 512, R("et"))
+    ttg(R("nr"), R("idt"), R("nl"), R("gg"), O.is_lt)
     turn(R("zt"), R("zr"))
-    gather(R("nr"), R("idt"), R("nl"))
     ev, od = R("z2", 0, 32, 0, 32, 2), R("z2", 1, 32, 0, 32, 2)
-    tt(R("z1", 0, 32, 0, 64), R("zt", 0, 512, 0, 64, 16), R("zt", 0, 512, 64, 128, 16), O.add)
-    tt(R("z2", 0, 32, 0, 32), R("z1", 0, 32, 0, 32), R("z1", 0, 32, 32, 64), O.add)
+    ts(R("tie"), R("nr"), -2.0 ** -100, None, O.mult)
+    tt(R("z2", 96, 128, 0, 64), R("zt", 0, 512, 0, 64, 16), R("zt", 0, 512, 64, 128, 16), O.add)
+    tt(R("z2", 0, 32, 0, 32), R("z2", 96, 128, 0, 32), R("z2", 96, 128, 32, 64), O.add)
     tt(R("z2", 32, 48, 0, 32), od, ev, O.subtract)
     ts(R("mk4"), R("c4"), p3, None, O.is_equal)
     ts(R("z2", 48, 64, 0, 32), R("z2", 32, 48, 0, 32), R("pf", 1, 2, 0, 32), None, O.mult)
-    memset(R("al", 0, 1), 1.0)
+    memset(R("alg", 0, 1), 1.0)
     tt(R("z2", 64, 96, 0, 32, 2), ev, R("z2", 48, 64, 0, 32), O.add)
     tt(R("z2", 65, 96, 0, 32, 2), od, R("z2", 48, 64, 0, 32), O.subtract)
-    pick("ex", EX * 3 + 128, EX * 3 + EX, "xq", 128, R("xl", 30, 39))
+    copy(R("bl"), R("ib"))
+    ts(R("bo"), R("bo0"), R("ca", 1, 2), None, O.add)
     for a in range(4):
-        copy(R("sf", 0, 32, 32 * a, 32 * a + 32), R("z2", 64, 96, 0, 32))
-    tt(R("c2d"), R("c2e"), R("c2f"), O.subtract)
+        copy(R("sf", 0, 32, 32 * a, 32 * a + 32), R("z2", 64, 96, 0, 32), "vs"[a % 2])
     copy(R("sw"), R("sf"))
     gather(R("sc"), R("sf"), R("pl", 0, 1))
-    for j in range(4):
-        ts(R("tie", 16 * j, 16 * j + 16), R("nr", 16 * j, 16 * j + 16), R("nc", 2 * j, 2 * j + 1), -2.0 ** -100, O.is_lt, O.mult)
-    ts(R("c2g", 0, 8, st=2), R("c2d", 0, 8, st=2), R("ca", 2, 3), None, O.mult)
-    ts(R("c2g", 1, 8, st=2), R("c2d", 1, 8, st=2), hcol, None, O.mult)
     ts(R("n1", 16, 24), R("sc", 0, 8), 1.0 / 8192, None, O.mult)
-    tt(R("c2"), R("c2g"), R("c2f"), O.add)
-    quant("wq", 0, 128, R("wt"))
 
     note(None, [R(n, UR, UW) for n in ("uc", "ucs")], [], "arc", count["arc"])
     for j in range(4):
-        pick("ex", EX * j, EX * j + 128, "uc", UW, R("sw", 8 * j, 8 * j + 8))
-    for j in range(4):
-        mm(BANKS[4 + j], 128, "ex", EX * j + 144, "ex", EX * j, EX * j + 128)
-        mm(BANKS[j], 136, "ex", EX * j, "ex", EX * j, EX * j + 136)
-    for j in range(4):
-        copy(R("cs", 128 * j, 128 * j + 128), R(BANKS[4 + j], 0, 128))
-        copy(R("cs", 512 + 8 * j, 520 + 8 * j), R(BANKS[j], 128, 136), "ssvv"[j])
-        copy(R("cg", 128 * j, 128 * j + 128), R(BANKS[j], 0, 128), "s")
-    gather(R("ss"), R("cs"), R("bl"))
-    row, own = R("ss", 0, 64), R("ss", 64, 128)
-    tt(R("dw"), row, own, O.subtract)
-    gather(R("gg"), R("cg"), R("bl", 0, 4))
-    tt(R("w2"), R("dw"), R("tie"), O.is_gt)
+        pick("ex", 128 * j, 128 * j + 128, "uc", UW, R("sw", 8 * j, 8 * j + 8))
+    for j, w in ((0, 1), (0, 0), (1, 1), (1, 0), (2, 1), (3, 1), (2, 0), (3, 0)):
+        mm(BANKS[4 * w + j], 128, "ex", 128 * j, "xq" if w else "ex", 0 if w else 128 * j, 128 if w else 128 * j + 128)
+        if w:
+            copy(R("cs", 32 * j, 32 * j + 32), R(BANKS[4 + j], 0, 32), "ssvv"[j])
+        else:
+            copy(R("cg", 128 * j, 128 * j + 128), R(BANKS[j], 0, 128), "s")
+    lin(R("ids"), R("idt"), 1.0 / 8192)
+    gather(R("ob"), R("cs"), R("bo"))
+    own = R("ob", 0, 128, st=2)
+    need("y", [], [R("ob")])
+    for s in ("", "s"):
+        dma("y", R("mg" + s, 0, P), R("vq" + s), "dmg", 2)
+    turn(R("obt"), R("ob"))
+    gather(R("gg"), R("cg"), R("bl"))
+    gather(R("row"), R("obt"), R("br"))
     tt(R("bb"), R("gg"), own, O.is_lt)
-    for j in range(4):
-        red(R("rk", j, j + 1), R("w2", 16 * j, 16 * j + 16), O.add)
-    tt(R("rk", 4, 8), R("rk", 0, 4), R("cst"), O.add)
-    ts(R("l2a", 0, 8, st=2), R("rk", 0, 4), R("ca", 5, 6), None, O.mult)
-    ts(R("l2a", 1, 8, st=2), R("rk", 0, 4), R("ca", 3, 4), None, O.mult)
-    copy(R("l1"), R("rk", 4, 8))
+    tt(R("dw"), R("row"), own, O.subtract)
+    tt(R("w2"), R("dw"), R("tie"), O.is_gt)
+    scan(R("rks", 0, 64), R("rst"), R("w2"), O.mult, O.add)
+    rank = R("rks", 15, 64, st=16)
+    tt(R("rks", 64, 68), rank, R("cst"), O.add)
+    ts(R("l2a", 0, 8, st=2), rank, R("ca", 5, 6), None, O.mult)
+    ts(R("l2a", 1, 8, st=2), rank, R("ca", 3, 4), None, O.mult)
+    copy(R("l1"), R("rks", 64, 68))
     tt(R("l2b"), R("l2a"), R("c2"), O.add)
     scatter(R("t1"), R("l1"), R("bb"))
     copy(R("l2"), R("l2b"))
     copy(R("t1", 15, 128, st=16), R("n1", 8, 16))
-    copy(R("t1", 14, 128, st=16), R("n1", 16, 24))
+    copy(R("t1", 14, 128, st=16), R("n1", 16, 24), "s")
     turn(R("t1t"), R("t1"))
     scatter(R("t2"), R("l2"), R("t1t"))
     for k in range(1, 4):
-        copy(R("t2", k, 256, st=4), R("t2", 0, 256, st=4))
+        copy(R("t2", k, 256, st=4), R("t2", 0, 256, st=4), "vvsv"[k])
     turn(R("t2t"), R("t2", 0, 256))
 
     def both(o, v, k):
         tt(o, R("t2t", 32 * v + k, 256, st=32), R("t2t", 32 * v + 16 + k, 256, st=32), O.add)
-    both(R("al", 1, 8), 1, 0)
+    both(R("alg", 9, 16), 1, 0)
     both(R("cu", 8, 14), 2, 1)
-    for u in range(1, 7):
-        w = 7 - u
-        ts(R("tmp", 8 * u, 8 * u + w), R("cu", 8 * u, 8 * u + w), R("al", u, u + 1), None, O.is_ge)
+    ts(R("tmp", 10, 16), R("cu", 8, 14), R("alg", 9, 10), None, O.is_ge)
+    both(R("cu", 16, 21), 3, 2)
+    both(R("nn"), 0, 15)
+    for u in range(2, 8):
+        if u < 7:
+            ts(R("tmp", 9 * u + 1, 8 * u + 8), R("cu", 8 * u, 8 * u + 7 - u), R("alg", 9 * u - 8, 9 * u - 7), R("tmp", 9 * u - 8, 9 * u - 7), O.is_ge, O.is_ge)
+        tt(R("alg", 9 * u, 8 * u + 8), R("alg", 9 * u - 8, 8 * u), R("tmp", 9 * u - 8, 8 * u), O.min)
         if u < 6:
             both(R("cu", 8 * u + 8, 8 * u + 14 - u), u + 2, u + 1)
-        else:
-            both(R("sl8"), 0, 14)
-        tt(R("al", u + 1, 8), R("al", u + 1, 8), R("tmp", 8 * u, 8 * u + w), O.min)
-        if u == 1:
-            both(R("nn"), 0, 15)
         if u == 2:
             ts(R("mk8"), R("nn"), R("ca", 8, 9), None, O.add)
-    scan(R("cn"), R("al"))
-    tt(R("ck"), R("cn"), R("al"), O.mult)
-    tt(R("z8"), R("ck"), R("mk8"), O.add)
-    red(R("nlv"), R("z8"), O.min, True)
-    ts(R("nls"), R("nlv"), 8192.0, 1551.0, O.mult, O.min)
-    spread("kl", 1, "nls", 0, 1, qs="vsvsvsvsvsvsvsvv")
-    send([(q, R("kl"), R("kla", 4 * here[q], 4 * here[q] + 4)) for q in others], "ark")
-
-    def rowsum(o, off, k):
-        op("v", lambda: g.vector.tensor_tensor(o["ap"], R("idt")["ap"].indirect(off["ap"]), k["ap"], O.add), [o], [R("idt"), off, k])
+        if u == 6:
+            both(R("sl8"), 0, 14)
+    al = R("alg", 0, 64, st=9)
+    scan(R("cn"), al, al, O.add, O.max)
+    tt(R("ck"), R("mk8"), al, O.mult)
     ts(R("ms8"), R("sl8"), R("ca", 8, 9), None, O.add)
-    rowsum(R("vr", 0, 64), R("kl"), R("key", 0, 64))
-    for k in range(6):
-        act(R("abo", 64 * k, 64 * k + 64), R("vr", 0, 64), AF.Abs, bias=R("cc", k, k + 1))
-    quant("eq", 0, 512, R("et"))
-    for ch in range(2):
-        for b in range(4):
-            mm(BANKS[4 * ch + b], 192, "eq", 128 * b, "vq", 192 * ch, 192 * ch + 192, True, False)
-    tt(R("y8"), R("ck"), R("ms8"), O.add)
-    ts(R("kt"), R("nlv"), 0.5, 8192.0, O.is_lt, O.mult)
+    tt(R("z8"), R("cn"), R("ck"), O.add)
+    red(R("nlv"), R("z8"), O.min, True)
+    ts(R("kl", 0, 1), R("nlv"), 8192.0, R("ca", 4, 5), O.mult, O.min)
+    ts(R("own"), R("pm"), R("nlv"), None, O.add)
+    ts(R("nls"), R("nlv"), 8192.0, R("ca", 4, 5), O.mult, O.min)
+    ttg(R("same"), R("ids"), R("kl", 0, 1), R("own"), O.is_equal)
+    tt(R("ms9"), R("ms8"), al, O.mult)
+    red(R("dup"), R("same"), O.max)
+    tt(R("y8"), R("cn"), R("ms9"), O.add)
+    ts(R("kd", 0, 1), R("dup"), R("ca", 4, 5), R("nls"), O.mult, O.max)
+    send([(q, R("kd"), R("kla", 2 * here[q], 2 * here[q] + 2)) for q in others], "ark")
+
+    parts = [(ch, b) for ch in range(2) for b in range(4)]
+    for ch, b in parts:
+        mm(BANKS[4 * ch + b], CUT[ch][1] - CUT[ch][0], "eq", 128 * b, "vq", CUT[ch][0], CUT[ch][1], True, False)
+    scatter(R("wo"), R("kd", 0, 1), R("ptv", 16 * r, 16 * r + 16))
     red(R("slv"), R("y8"), O.min, True)
-    tt(R("kv"), R("nlv"), R("kt"), O.mult)
     ts(R("yv"), R("slv"), 0.5, 8192.0, O.is_lt, O.mult)
-    ts(R("zz", 64, 68), R("mk4"), R("kv"), None, O.mult)
+    turn(R("tko"), R("wo", P * r, P * r + P))
     tt(R("zz", 96, 97), R("slv"), R("yv"), O.mult)
-    for k in range(2):
-        red(R("ab", 200 * k + 192, 200 * k + 193), R("abo", 64 * k, 64 * k + 64), O.min)
     turn(R("yr"), R("zz", 96, 128))
-    red(R("ab", 592, 593), R("abo", 128, 192), O.min)
+    tt(R("wown"), R("tko", 0, P, st=32), R("tko", 16, P, st=32), O.min)
     gather(R("yd"), R("yr"), R("hv"))
-    red(R("ab", 792, 793), R("abo", 192, 256), O.min)
     turn(R("ydt"), R("yd"))
-    for k in range(4, 6):
-        red(R("ab", 200 * k + 192, 200 * k + 193), R("abo", 64 * k, 64 * k + 64), O.min)
+    for a in range(4):
+        for b in range(4):
+            copy(R("ksl", 2 * a, 2 * a + 2, 32 * b, 32 * b + 32), R("ydt", 0, 64, 32 * a, 32 * a + 32, 32), "s")
 
     note(None, [R("kla")], [], "ark", count["ark"])
-    vo = R("vr", 64, 256)
-    rowsum(vo, R("kla"), R("key", 64, 256))
-    for k in range(4):
-        act(R("ab", 200 * k, 200 * k + 192), vo, AF.Abs, bias=R("cc", k, k + 1))
-    spread("ksl", 2, "ydt", 0, 64, 32, 0, 3, "s")
-    for k in (4, 5):
-        ts(R("ab", 200 * k, 200 * k + 192), vo, R("cc", k, k + 1), None, O.add)
-    for k in (4, 5, 0, 1, 2, 3):
-        red(R("zz", 32 + k, 33 + k), R("ab", 200 * k, 200 * k + 193), O.min, True)
+    for k, q in reversed(list(enumerate(others))):
+        scatter(R("wk"), R("kla", 2 * k, 2 * k + 1), R("ptv", 16 * q, 16 * q + 16))
+        if k == 2:
+            ts(R("kt"), R("nlv"), 0.5, None, O.is_lt)
+        if k == 1:
+            ts(R("kw"), R("nlv"), 8192.0, 1.0, O.mult, O.add)
+    tt(R("kv"), R("kw"), R("kt"), O.mult)
+    turn(R("tk"), R("wk", P * r, P * r + P))
+    ts(R("zz", 64, 68), R("mk4"), R("kv"), None, O.mult)
+    tt(R("wa"), R("tk", 0, P, st=32), R("tk", 16, P, st=32), O.min)
+    pick("kq", 0, 64, "uc", UW, R("ksl", 0, 4))
+    tt(R("wb"), R("wa"), R("wown"), O.min)
     turn(R("kpt"), R("zz", 64, 96))
-    turn(R("rpt"), R("zz", 32, 64))
+    tt(R("wc", 0, 12, 0, 64), R("wb", 0, 12, 0, 64), R("wb", 0, 12, 64, 128), O.min)
+    for a in range(4):
+        tt(R("zz", 32, 44, 32 * a, 32 * a + 32), R("wc", 0, 12, 0, 32), R("wc", 0, 12, 32, 64), O.min)
+    turn(R("lr"), R("zz", 32, 64))
+    pick("kq", 64, 128, "uc", UW, R("ksl", 4, 8))
+    gather(R("ld"), R("lr"), R("hv"))
     tt(R("kp2"), R("kpt", 0, 32, st=2), R("kpt", 1, 32, st=2), O.add)
-    for k in range(2):
-        tt(R("dmn", 16 * k, 16 * k + 16), R("rpt", 0, 16), R("rpt", 16, 32), O.min)
+    turn(R("ldt"), R("ld"))
     tt(R("kp3"), R("kp2", 0, 16, st=2), R("kp2", 1, 16, st=2), O.add)
-    turn(R("lc"), R("dmn"))
+    copy(R("ln", 0, 24, st=2), R("ldt", 0, 12))
+    copy(R("ln", 1, 24, st=2), R("ldt", 32, 44), "s")
     ts(R("kpo"), R("kp3"), -1.0, None, O.add)
-    ts(R("lcs"), R("lc", 0, 6), 256.0, 128.0, O.mult, O.min)
     for a in range(4):
         dma("y", T.kp[:, 8 * a:8 * a + 8], R("kpo", 0, 8, 32 * a, 32 * a + 4), "dk", 4)
 
     note(None, [R("xa" + s, 32 * q, 32 * q + 32) for q in others for s in ("", "s")], [], "arx", count["arx"])
-    for ch in range(2):
-        spread("ln", 6, "lcs", 0, 6, lo=2 * ch, hi=2 * ch + 2, qs="vsvvsvsv")
-        pick("qp", 192 * ch, 192 * ch + 192, "xa", 160, R("ln", 12 * ch, 12 * ch + 12))
-    for ch in range(2):
-        for b in range(4):
-            mm(BANKS[4 * ch + b], 192, "eq", 128 * b, "qp", 192 * ch, 192 * ch + 192, False, True)
-    ts(R("sl0"), R("ln"), 127.5, 384.0, O.is_lt, O.mult)
-    spread("ksl", 2, "ydt", 0, 64, 32, 3, 4, "v")
+    for a, b in CUT:
+        pick("qp", a, b, "xa", 160, R("ln", a // 16, b // 16))
+    for ch, b in parts:
+        mm(BANKS[4 * ch + b], CUT[ch][1] - CUT[ch][0], "eq", 128 * b, "qp", CUT[ch][0], CUT[ch][1], False, True)
+    ts(R("sl0"), R("ln"), N * A - 0.5, float(P), O.is_lt, O.mult)
     tt(R("sl1"), R("sl0"), R("jc"), O.add)
 
     def half(ch, bs):
         for b in bs:
-            copy(R("nt", 768 * ch + b, 768 * ch + 768, st=4), R(BANKS[4 * ch + b], 0, 192), "sv"[b % 2])
+            copy(R("nt", 4 * CUT[ch][0] + b, 4 * CUT[ch][1], st=4), R(BANKS[4 * ch + b], 0, CUT[ch][1] - CUT[ch][0]), "sv"[b % 2])
 
     def new(ch):
-        quant("mg", P + 192 * ch, P + 192 * ch + 192, R("nt", 768 * ch, 768 * ch + 768))
+        quant("mg", P + CUT[ch][0], P + CUT[ch][1], R("nt", 4 * CUT[ch][0], 4 * CUT[ch][1]))
 
     def store(ch, late):
-        pick("oq", 192 * ch, 192 * ch + 192, "mg", 2 * P, R("sl", 12 * ch, 12 * ch + 12))
-        dma("y", T.oc[:, 768 * ch:768 * ch + 768], R("oq", 192 * ch, 192 * ch + 192), "do%d" % ch, 1)
+        a, b = CUT[ch]
+        pick("oq", a, b, "mg", 2 * P, R("sl", a // 16, b // 16))
+        dma("y", T.oc[:, 4 * a:4 * b], R("oq", a, b), "do%d" % ch, 1)
         for k in range(4):
-            dma("sy"[k % 2] if late else "y", T.osc[4 * k:4 * k + 4, 192 * ch:192 * ch + 192], R("oqs", 192 * ch, 192 * ch + 192, 32 * k, 32 * k + 4), "dp%d" % ch, 4)
-    half(0, (0, 1, 2))
+            dma("sy"[k % 2] if late else "y", T.osc[4 * k:4 * k + 4, a:b], R("oqs", a, b, 32 * k, 32 * k + 4), "dp%d" % ch, 4)
+    half(0, (0, 1))
     copy(R("sl"), R("sl1"))
-    pick("kq", 0, 128, "uc", UW, R("ksl"), "v")
-    half(0, (3,))
-    pick("kq", 0, 128, "uc", UW, R("ksl"), "s")
+    half(0, (2, 3))
     mm(BANKS[0], 128, "wq", 0, "kq", 0, 128)
     new(0)
     half(1, (0, 2))

from concourse.bass import DstId, RemoteDMATransfer
from concourse.mybir import dt, AluOpType, AxisListType, ActivationFunctionType

N, P, A, C, LC = 4, 384, 32, 16, 160
UB = 32
UR = UB + P
UW = UR + 3 * LC
MO = 3 * P
MW = MO + 4 * P
DB = P
DUMP = N * P + 4
IW = DUMP + 20
CUT = ((0, 160), (160, 384))

F32, BF, I32, U16, U8, F8 = "float32", "bfloat16", "int32", "uint16", "uint8", "float8_e4m3fn_x4"
SCRATCH = {}
for _d, _names in (
    (BF, "tbt:1536 xt:512 wt:512 et:2048 nt:1536"),
    (F8, "vq:384 xq:128 wq:128 eq:512 xa:160 uc:896 pk:480 ex:512 kq:128 qp:384 mg:768 oq:384"),
    (U8, "vqs:384 xqs:128 wqs:128 eqs:512 xas:160 ucs:896 pks:480 exs:512 kqs:128 qps:384 mgs:768 oqs:384"),
    (I32, "kci:64"), (U16, "bl:4 bo:8 br:4 pl:2 rl:24 hv:4"), (BF, "ones:16 eye:128 ptv:64"),
    (F32, "kcf:512 idt:1560 ids:1560 cv:192 zz:128"),
    (I32, "cdh:16 cdi:32"), (U16, "off:32 wl:12 lst:10 lnd:30 ls:30"), (BF, "mk0:2688 mk1:2688 tm:768 m1:24"),
    (F32, "req:192 x0:32 xt0:32 wn:1152 wnt:160 lr:32 ld:64 ldt:64"),
    (F32, "cdp:32 zp:12 zrep:384 zf:416 gx:128 zr:512 zt:512 z2:128 sf:32 sc:16 nc:16 n1:24 nr:64 tie:64"), (U16, "og:32 sw:32 nl:4 kl:2"),
    (F32, "cs:128 cg:512 ob:128 obt:128 row:64 gg:64 dw:64 w2:64 bb:64 rks:68 l2a:8 l2b:8 t1:128 t1t:128 t2:640 t2t:256 cu:64 tmp:64 alg:64"), (U16, "l1:4 l2:8"),
    (F32, "pr:160 kpt:32 yr:32 yd:64 ydt:64 yt:128"), (U16, "kd:2 ksl:8 kla:6"),
    (BF, "wk:1568 wo:1568 tk:384 tko:384"), (F32, "wm:64 sl0:24 sl1:24"), (U16, "ln:24 sl:24"),
):
    for _n in _names.split():
        SCRATCH[_n.split(":")[0]] = ("sbuf", [128, int(_n.split(":")[1])], _d)
PART = {}
for _d, _names in (
    ("kcf", "pf:8 cq:8 ca:12 t32:32 tri:32 dc0:12 dc:12 dc1:12 plc:12 c4:4 bo0:8 br0:4 br1:4 hv0:4 c2:8 cst0:4 cst:4 jc0:24 jc:24 mk4:4 rst0:64 rst:64 pm0:16 pm:16 pt0:64"),
    ("kci", "ip:2 ib:4 it:8 ir:24"),
    ("req", "mm:12 tot:1 base:1 sn:12 g1:12 g2:12 g3:12"),
    ("pr", "nn:8 sl8:8 mk8:8 ms8:8 ms9:8 cn:8 ck:8 z8:8 y8:8 nlv:1 nls:1 slv:1 kt:1 kw:1 kv:1 yv:1 kp2:16 kp3:8 kpo:8 own:16 same:16 dup:1"),
    ("wm", "wa:12 wb:12 wc:12 wown:12"),
):
    _c = 0
    for _n in _names.split():
        PART[_n.split(":")[0]] = (_d, _c, int(_n.split(":")[1]))
        _c += PART[_n.split(":")[0]][2]
    assert _c <= SCRATCH[_d][1][1]
BANKS = ["pb%d" % _b for _b in range(8)]
for _n in BANKS:
    SCRATCH[_n] = ("psum", [128, 512], F32)
SEMAPHORES = ["ev", "ec", "et_", "ep", "dch", "dcd", "dx", "dtb", "dw", "dxa", "dmg", "dz", "dk", "dy", "do0", "do1", "dp0", "dp1",
              "arx", "arl", "arc", "ark", "loc"]


def rank_program(g, core, T, topo):
    r = T.rank_of(core)
    if r is None:
        return
    O, AF, X = AluOpType, ActivationFunctionType, AxisListType.X
    eng = {"v": g.vector, "s": g.scalar, "t": g.tensor, "p": g, "y": g.sync}
    semof = {"v": "ev", "s": "ec", "t": "et_", "p": "ep"}
    count = {}
    known = {k: {} for k in eng}
    log = {}

    def R(name, c0=0, c1=None, p0=0, p1=128, st=1):
        name, base, n = PART.get(name, (name, 0, SCRATCH[name][1][1] if name in SCRATCH else 0))
        c0, c1 = base + c0, base + (n if c1 is None else c1)
        ap = T[name][p0:p1, c0:c1] if st == 1 else T[name][p0:p1, c0:c1:st]
        return {"n": name, "c0": c0, "c1": c1, "p0": p0, "p1": p1, "st": st, "ap": ap}

    def meet(a, b):
        if a["p1"] <= b["p0"] or b["p1"] <= a["p0"] or a["c1"] <= b["c0"] or b["c1"] <= a["c0"]:
            return False
        return not (a["st"] == b["st"] and a["st"] > 1 and (a["c0"] - b["c0"]) % a["st"])

    def need(q, outs, ins, skip=None):
        todo = {}
        for kind, regs in (("w", outs), ("r", ins)):
            for x in regs:
                bank = x["n"] in BANKS
                for y, k, tok in log.get(x["n"], []):
                    if (skip is not None and tok[3] == skip) or known[q].get(tok[0], 0) >= tok[1]:
                        continue
                    if bank:
                        hit = tok[0] != semof.get(q) or (q != "t" and meet(x, y) and "w" in (kind, k))
                    else:
                        hit = "w" in (kind, k) and meet(x, y)
                    if hit and (tok[0] not in todo or todo[tok[0]][1] < tok[1]):
                        todo[tok[0]] = tok
        for s in sorted(todo):
            tok = todo[s]
            if known[q].get(s, 0) >= tok[1]:
                continue
            eng[q].wait_ge(T.sem[s], tok[1])
            for a, b in list(tok[2].items()) + [(s, tok[1])]:
                known[q][a] = max(known[q].get(a, 0), b)

    def note(q, outs, ins, sem, val, tag=None):
        tok = (sem, val, dict(known[q]) if q else {}, tag)
        for k, regs in (("w", outs), ("r", ins)):
            for x in regs:
                log.setdefault(x["n"], []).append((x, k, tok))

    def op(q, call, outs, ins):
        need(q, outs, ins)
        s = semof[q]
        count[s] = count.get(s, 0) + 1
        call().then_inc(T.sem[s], 1)
        note(q, outs, ins, s, count[s])

    def u8(x):
        return x["ap"].bitcast(dt.uint8) if SCRATCH[x["n"]][2] == F8 else x["ap"]

    def dma(q, o, i, sem, total):
        outs, ins = [x for x in (o,) if isinstance(x, dict)], [x for x in (i,) if isinstance(x, dict)]
        need(q, outs, ins, skip=sem)
        eng[q].dma_start(u8(o) if outs else o, u8(i) if ins else i).then_inc(T.sem[sem], 16)
        count[sem] = count.get(sem, 0) + 16
        note(q, outs, ins, sem, 16 * total, tag=sem)

    def memset(a, c):
        op("v", lambda: g.vector.memset(a["ap"], c), [a], [])

    def copy(o, i, q="v"):
        if q == "v":
            op("v", lambda: g.vector.tensor_copy(o["ap"], i["ap"]), [o], [i])
        else:
            op("s", lambda: g.scalar.activation(o["ap"], i["ap"], AF.Copy), [o], [i])

    def tt(o, a, b, f):
        op("v", lambda: g.vector.tensor_tensor(o["ap"], a["ap"], b["ap"], f), [o], [a, b])

    def ttg(o, win, off, b, f):
        op("v", lambda: g.vector.tensor_tensor(o["ap"], win["ap"].indirect(off["ap"]), b["ap"], f), [o], [win, off, b])

    def ts(o, a, s1, s2, f1, f2=None):
        ins = [a] + [s for s in (s1, s2) if isinstance(s, dict)]
        v1 = s1["ap"] if isinstance(s1, dict) else s1
        v2 = s2["ap"] if isinstance(s2, dict) else s2
        if f2 is None:
            op("v", lambda: g.vector.tensor_scalar(o["ap"], a["ap"], v1, None, f1), [o], ins)
        else:
            op("v", lambda: g.vector.tensor_scalar(o["ap"], a["ap"], v1, v2, f1, f2), [o], ins)

    def red(o, a, f, size=False):
        kw = {"apply_absolute_value": True} if size else {}
        op("v", lambda: g.vector.tensor_reduce(o["ap"], a["ap"], X, f, **kw), [o], [a])

    def scan(o, a, b, f1, f2):
        op("v", lambda: g.vector.tensor_tensor_scan(o["ap"], a["ap"], b["ap"], 0.0, f1, f2), [o], [a, b])

    def lin(o, a, scale=1.0, bias=0.0, f=AF.Identity):
        ins = [a] + [s for s in (scale, bias) if isinstance(s, dict)]
        kw = {"scale": scale["ap"] if isinstance(scale, dict) else scale, "bias": bias["ap"] if isinstance(bias, dict) else bias}
        op("s", lambda: g.scalar.activation(o["ap"], a["ap"], f, **kw), [o], ins)

    def turn(o, a):
        op("v", lambda: g.vector.transpose(o["ap"], a["ap"]), [o], [a])

    def gather(o, win, off, q="v"):
        if q == "v":
            op("v", lambda: g.vector.tensor_copy(o["ap"], win["ap"].indirect(off["ap"])), [o], [win, off])
        else:
            op("s", lambda: g.scalar.activation(o["ap"], win["ap"].indirect(off["ap"]), AF.Copy), [o], [win, off])

    def scatter(win, off, i):
        op("v", lambda: g.vector.tensor_copy(win["ap"].indirect(off["ap"]), i["ap"]), [win], [off, i])

    def pick(cn, o0, o1, wn, w1, off):
        o, w = R(cn, o0, o1), R(wn, 0, w1)
        op("v", lambda: g.vector.tensor_copy(o["ap"].bitcast(dt.uint32), w["ap"].bitcast(dt.uint32).indirect(off["ap"])), [o], [w, off])
        gather(R(cn + "s", o0, o1), R(wn + "s", 0, w1), off, "s")

    def quant(cn, c0, c1, tile):
        o, s = R(cn, c0, c1), R(cn + "s", c0, c1)
        op("v", lambda: g.vector.quantize_mx(o["ap"], s["ap"], tile["ap"]), [o, s], [tile])

    def mm(bank, n, a, a0, b, b0, b1, start=True, stop=True):
        o, l, ls, m, ms = R(bank, 0, n), R(a, a0, a0 + 128), R(a + "s", a0, a0 + 128), R(b, b0, b1), R(b + "s", b0, b1)
        op("t", lambda: g.tensor.matmul_mx(o["ap"], l["ap"], ls["ap"], m["ap"], ms["ap"], start, stop), [o], [l, ls, m, ms])

    def iota(name, pattern, base, cm, c0=0, c1=None):
        o = R(name, c0, c1)
        kw = {"allow_small_or_imprecise_dtypes": True} if SCRATCH[o["n"]][2] in (F32, BF) else {}
        op("p", lambda: g.iota(o["ap"], pattern, base, cm, **kw), [o], [])

    others = [q for q in range(N) if q != r]
    here = {q: (r if r < q else r - 1) for q in others}

    def send(pieces, sem, turned=0):
        need("p", [], [s for _q, s, _d in pieces])
        parts = 1 if len(pieces) == 1 else 4
        tr = []
        for k, (q, s, d) in enumerate(pieces):
            e = topo.engines(core, T.cores[q])
            m = len(e) // parts
            k4 = (k + turned) % parts
            rid, pid, _s = topo.addr(T.cores[q])
            tr.append(RemoteDMATransfer(dst_ids=[DstId(rid=rid, pnc=pid)], dma_engine_mask=sum(1 << n for n in e[k4 * m:k4 * m + m]),
                                        remote_sem=T.sem[sem], src=u8(s), dst=u8(d)))
            count["loc"] = count.get("loc", 0) + m
            count[sem] = count.get(sem, 0) + m
        g.remote_dma_fused(tr, local_sem=T.sem.loc)

    for k in range(8):
        dma("ys"[k % 2], R("cdh", 0, 16, 16 * k, 16 * k + 16), T.cd[:, 16 * (k % 2):16 * (k % 2) + 16], "dch", 8)
    dma("y", R("xt", 0, 128), T.x[:, :], "dx", 1)
    dma("y", R("tbt"), T.tb[:, :], "dtb", 1)
    for k in range(8):
        dma("y", R("cdi", 0, 32, 16 * k, 16 * k + 16), T.cd[:, :], "dcd", 8)
    dma("y", R("wt"), T.w[:, :], "dw", 1)

    IQ = IW // 4
    iota("ip", [[1, 1]], 0, 1, 0, 1)
    iota("t32", [[1, 32]], 0, 0)
    iota("dc0", [[1, 12]], DB, 0)
    iota("cv", [[32, 12], [1, 16]], 0, 0)
    iota("idt", [[1, IQ]], 0, 0, 0, IQ)
    iota("hv0", [[16, 2], [0, 2]], 0, 0)
    iota("plc", [[32, 12]], UB - 32 * r, 1)
    iota("ir", [[1, 12], [0, 2]], 0, 0)
    iota("c4", [[1, 4]], 0, 0)
    memset(R("mk0", MO, MO + P), 0.0)
    p = R("ip", 0, 1)
    for k, (sh, msk) in enumerate(((0, 15), (4, 1), (0, 7), (4, 7), (0, 3), (5, 3), (0, 31), (1, 3))):
        ts(R("it", k, k + 1), p, sh, msk, O.logical_shift_right, O.bitwise_and)
    memset(R("mk1", MO, MO + P), 0.0)
    copy(R("pf", 0, 8), R("it", 0, 8))
    lcol, hcol, _ecol, gcol, p3, acol, pcol, bcol = [R("pf", k, k + 1) for k in range(8)]
    memset(R("ones"), 1.0)
    ts(R("cq", 0, 1), acol, float(-P), float(MO), O.mult, O.add)
    memset(R("xt", 128, 512), 0.0)
    ts(R("tri"), R("t32"), pcol, None, O.is_gt)
    lin(R("ca", 0, 1), hcol, 16.0)
    lin(R("ca", 6, 7), pcol, 12.0)
    lin(R("dc"), R("dc0"), 1.0, R("ca", 6, 7))
    lin(R("cv"), R("cv"), 1.0, R("ca", 0, 1))
    lin(R("dc1"), R("dc"), 1.0, 1.0)
    memset(R("wn", 0, LC), 0.0)
    ts(R("off", 0, 32, st=2), R("cdh"), R("cq", 0, 1), None, O.add)

    for i in range(A // 2):
        scatter(R("mk%d" % (i % 2)), R("off", 2 * i, 2 * i + 1), R("ones"))
    for k in range(2):
        turn(R("tm", P * k, P * k + P), R("mk%d" % k, MO, MO + P))

    quant("xq", 0, 128, R("xt"))
    for s, k in (("", 0), ("s", 3)):
        send([(q, R("xq" + s, 0, 32), R("xa" + s, 32 * r, 32 * r + 32)) for q in others], "arx", k)
    for s in ("", "s"):
        dma("y", R("uc" + s, 0, 32), R("xq" + s, 32, 64), "dz", 2)
        dma("y", R("xa" + s, 32 * r, 32 * r + 32), R("xq" + s, 0, 32), "dxa", 4)
        dma("y", R("xa" + s, 128, 160), R("xq" + s, 32, 64), "dxa", 4)

    lin(R("cq", 1, 2), acol, float(-P), 16.0)
    lin(R("ca", 1, 2), gcol, 4.0)
    lin(R("ca", 4, 5), lcol, 1.0, float(DUMP))
    lin(R("ca", 2, 3), hcol, -1.0, 1.0)
    lin(R("ca", 3, 4), hcol, 32.0)
    lin(R("ca", 5, 6), hcol, -32.0, 32.0)
    lin(R("ca", 8, 9), p3, -1.0, -1.0)
    for k in range(8):
        lin(R("et", 256 * k, 256 * k + 256), R("idt", 0, 256), 0.0)
    eye, nil = R("eye"), R("et", 0, 128)
    op("p", lambda: g.affine_select(eye["ap"], nil["ap"], [[1, 128]], O.not_equal, 0.5, 0, -1), [eye], [nil])
    for k in range(1, 4):
        lin(R("idt", IQ * k, IQ * k + IQ), R("idt", 0, IQ), 1.0, float(IQ * k))
    for j in range(4):
        copy(R("cdp", 8 * j, 8 * j + 8), R("cdi", j, 32, st=4), "s")
    for b in range(4):
        copy(R("et", 513 * b, 512 * b + 512, st=4), eye, "s")
    tt(R("m1"), R("tm", 0, 2 * P, st=32), R("tm", 16, 2 * P, st=32), O.max)
    ts(R("hv"), R("hv0"), lcol, None, O.add)
    tt(R("mm"), R("m1", 0, 12), R("m1", 12, 24), O.max)
    memset(R("zf", 0, 16), 0.0)
    red(R("tot"), R("mm"), O.add)
    scan(R("sn"), R("mm"), R("mm"), O.add, O.max)
    ts(R("x0"), R("tri"), R("tot"), None, O.mult)
    tt(R("g1"), R("sn"), R("dc1"), O.subtract)
    turn(R("xt0"), R("x0"))
    tt(R("g2"), R("g1"), R("mm"), O.mult)
    red(R("base"), R("xt0"), O.add)
    tt(R("g3"), R("g2"), R("dc"), O.add)
    ts(R("cq", 3, 4), acol, float(r), float(-LC), O.is_gt, O.mult)
    ts(R("wl"), R("g3"), R("base"), None, O.add)
    ts(R("cq", 2, 3), acol, float(LC), R("cq", 3, 4), O.mult, O.add)
    scatter(R("wn"), R("wl"), R("cv"))
    ts(R("zp"), R("sn"), R("base"), R("cq", 2, 3), O.add, O.add)
    turn(R("wnt"), R("wn", 0, LC))
    memset(R("zz"), 0.0)
    tt(R("zz", 0, 5), R("wnt", 0, LC, st=32), R("wnt", 16, LC, st=32), O.add)
    ts(R("zp"), R("zp"), float(UR - 1), None, O.add)
    turn(R("lr"), R("zz", 0, 32))
    copy(R("zp", 0, 12, 32 * r, 32 * r + 32), R("plc", 0, 12, 32 * r, 32 * r + 32))
    gather(R("ld"), R("lr"), R("hv"))
    copy(R("rl"), R("ir"))
    turn(R("ldt"), R("ld"))
    for k in range(2):
        copy(R("lst", k, 10, st=2), R("ldt", 32 * k, 32 * k + 5), "vs"[k])
    send([(q, R("lst"), R("lnd", 10 * here[q], 10 * here[q] + 10)) for q in others], "arl")

    gather(R("zrep"), R("zp"), R("rl"), "s")
    iota("br0", [[32, 4]], 0, 0)
    iota("rst0", [[0, 4], [1, 16]], 0, 0)
    iota("pm0", [[4, 4], [0, 4]], 3, 0)
    iota("ib", [[128, 4]], 0, 1)
    iota("bo0", [[33, 4], [0, 2]], 0, 0)
    iota("cst0", [[32, 4]], 0, 0)
    iota("pt0", [[A, N], [1, 4], [0, 4]], 0, 0)
    iota("jc0", [[16, 24]], 0, 0)
    quant("vq", 0, P, R("tbt"))
    memset(R("zf", 400, 416), 0.0)
    quant("uc", UB, UR, R("tbt"))
    ts(R("gx", 0, 32), R("cdp"), R("cq", 1, 2), 15.0, O.add, O.max)
    turn(R("zf", 16, 400), R("zrep"))
    tt(R("gx", 32, 64, st=2), R("gx", 1, 32, st=2), R("gx", 0, 32, st=2), O.subtract)
    tt(R("gx", 33, 64, st=2), R("gx", 0, 32, st=2), R("gx", 1, 32, st=2), O.subtract)
    ts(R("pl", 0, 1), bcol, 8.0, gcol, O.mult, O.add)
    ts(R("gx", 64, 96), R("gx", 32, 64), hcol, None, O.mult)
    gather(R("nc"), R("cdp"), R("pl", 0, 1))
    tt(R("gx", 96, 128), R("gx", 64, 96), R("gx", 0, 32), O.add)
    ts(R("og"), R("gx", 96, 128), 400.0, None, O.min)

    note(None, [R("lnd", 0, 30)], [], "arl", count["arl"])
    for a in range(4):
        copy(R("ls", 0, 30, 32 * a, 32 * a + 32), R("lnd", 0, 30, 32 * r, 32 * r + 32), "vs"[a % 2])
    for k, q in enumerate(others):
        pick("pk", LC * k, LC * k + LC, "vq", P, R("ls", 10 * k, 10 * k + 10))
        send([(q, R("pk", LC * k, LC * k + LC), R("uc", UR + LC * here[q], UR + LC * here[q] + LC))], "arc")
    send([(q, R("pks", LC * k, LC * k + LC), R("ucs", UR + LC * here[q], UR + LC * here[q] + LC)) for k, q in enumerate(others)], "arc", 3)

    iota("t1", [[0, 128]], 0, 0)
    iota("t2", [[0, 256]], 0, 0, 0, 256)
    for n in ("wk", "wo"):
        iota(n, [[0, P]], N * A, 0, P * r, P * r + P)
    lin(R("br1"), R("br0"), 1.0, R("ca", 0, 1))
    for j in range(4):
        lin(R("gg", 16 * j, 16 * j + 16), R("t32", 0, 16), 0.0, R("nc", 2 * j, 2 * j + 1))
    gather(R("zr"), R("zf"), R("og"), "s")
    lin(R("cst"), R("cst0"), 1.0, R("ca", 0, 1))
    lin(R("n1", 8, 16), R("nc", 0, 8), 1.0 / 8192)
    lin(R("jc"), R("jc0"), 1.0, lcol)
    lin(R("ptv"), R("pt0"), 1.0, R("ca", 1, 2))
    lin(R("ca", 7, 8), hcol, 28.0, 4.0)
    lin(R("ca", 9, 10), hcol, -28.0, 32.0)
    lin(R("ca", 10, 11), hcol, 512.0)
    lin(R("ca", 11, 12), hcol, -512.0, 528.0)
    lin(R("cq", 4, 5), lcol, hcol, R("ca", 10, 11))
    lin(R("cq", 5, 6), lcol, R("ca", 2, 3), R("ca", 11, 12))
    lin(R("c2", 0, 8, st=2), R("c4"), R("ca", 7, 8), R("cq", 4, 5))
    lin(R("c2", 1, 8, st=2), R("c4"), R("ca", 9, 10), R("cq", 5, 6))

    copy(R("nl"), R("nc", 0, 8, st=2))
    ts(R("br"), R("br1"), lcol, None, O.add)
    ts(R("rst"), R("rst0"), 0.5, None, O.is_gt)
    ts(R("pm"), R("pm0"), lcol, 4096.0, O.is_ge, O.mult)
    memset(R("kd"), 0.0)
    quant("wq", 0, 128, R("wt"))
    quant("eq", 0, 512, R("et"))
    ttg(R("nr"), R("idt"), R("nl"), R("gg"), O.is_lt)
    turn(R("zt"), R("zr"))
    ev, od = R("z2", 0, 32, 0, 32, 2), R("z2", 1, 32, 0, 32, 2)
    ts(R("tie"), R("nr"), -2.0 ** -100, None, O.mult)
    tt(R("z2", 96, 128, 0, 64), R("zt", 0, 512, 0, 64, 16), R("zt", 0, 512, 64, 128, 16), O.add)
    tt(R("z2", 0, 32, 0, 32), R("z2", 96, 128, 0, 32), R("z2", 96, 128, 32, 64), O.add)
    tt(R("z2", 32, 48, 0, 32), od, ev, O.subtract)
    ts(R("mk4"), R("c4"), p3, None, O.is_equal)
    ts(R("z2", 48, 64, 0, 32), R("z2", 32, 48, 0, 32), R("pf", 1, 2, 0, 32), None, O.mult)
    memset(R("alg", 0, 1), 1.0)
    tt(R("z2", 64, 96, 0, 32, 2), ev, R("z2", 48, 64, 0, 32), O.add)
    tt(R("z2", 65, 96, 0, 32, 2), od, R("z2", 48, 64, 0, 32), O.subtract)
    copy(R("bl"), R("ib"))
    ts(R("bo"), R("bo0"), R("ca", 1, 2), None, O.add)
    for a in range(4):
        copy(R("sf", 0, 32, 32 * a, 32 * a + 32), R("z2", 64, 96, 0, 32), "vs"[a % 2])
    copy(R("sw"), R("sf"))
    gather(R("sc"), R("sf"), R("pl", 0, 1))
    ts(R("n1", 16, 24), R("sc", 0, 8), 1.0 / 8192, None, O.mult)

    note(None, [R(n, UR, UW) for n in ("uc", "ucs")], [], "arc", count["arc"])
    for j in range(4):
        pick("ex", 128 * j, 128 * j + 128, "uc", UW, R("sw", 8 * j, 8 * j + 8))
    for j, w in ((0, 1), (0, 0), (1, 1), (1, 0), (2, 1), (3, 1), (2, 0), (3, 0)):
        mm(BANKS[4 * w + j], 128, "ex", 128 * j, "xq" if w else "ex", 0 if w else 128 * j, 128 if w else 128 * j + 128)
        if w:
            copy(R("cs", 32 * j, 32 * j + 32), R(BANKS[4 + j], 0, 32), "ssvv"[j])
        else:
            copy(R("cg", 128 * j, 128 * j + 128), R(BANKS[j], 0, 128), "s")
    lin(R("ids"), R("idt"), 1.0 / 8192)
    gather(R("ob"), R("cs"), R("bo"))
    own = R("ob", 0, 128, st=2)
    need("y", [], [R("ob")])
    for s in ("", "s"):
        dma("y", R("mg" + s, 0, P), R("vq" + s), "dmg", 2)
    turn(R("obt"), R("ob"))
    gather(R("gg"), R("cg"), R("bl"))
    gather(R("row"), R("obt"), R("br"))
    tt(R("bb"), R("gg"), own, O.is_lt)
    tt(R("dw"), R("row"), own, O.subtract)
    tt(R("w2"), R("dw"), R("tie"), O.is_gt)
    scan(R("rks", 0, 64), R("rst"), R("w2"), O.mult, O.add)
    rank = R("rks", 15, 64, st=16)
    tt(R("rks", 64, 68), rank, R("cst"), O.add)
    ts(R("l2a", 0, 8, st=2), rank, R("ca", 5, 6), None, O.mult)
    ts(R("l2a", 1, 8, st=2), rank, R("ca", 3, 4), None, O.mult)
    copy(R("l1"), R("rks", 64, 68))
    tt(R("l2b"), R("l2a"), R("c2"), O.add)
    scatter(R("t1"), R("l1"), R("bb"))
    copy(R("l2"), R("l2b"))
    copy(R("t1", 15, 128, st=16), R("n1", 8, 16))
    copy(R("t1", 14, 128, st=16), R("n1", 16, 24), "s")
    turn(R("t1t"), R("t1"))
    scatter(R("t2"), R("l2"), R("t1t"))
    for k in range(1, 4):
        copy(R("t2", k, 256, st=4), R("t2", 0, 256, st=4), "vvsv"[k])
    turn(R("t2t"), R("t2", 0, 256))

    def both(o, v, k):
        tt(o, R("t2t", 32 * v + k, 256, st=32), R("t2t", 32 * v + 16 + k, 256, st=32), O.add)
    both(R("alg", 9, 16), 1, 0)
    both(R("cu", 8, 14), 2, 1)
    ts(R("tmp", 10, 16), R("cu", 8, 14), R("alg", 9, 10), None, O.is_ge)
    both(R("cu", 16, 21), 3, 2)
    both(R("nn"), 0, 15)
    for u in range(2, 8):
        if u < 7:
            ts(R("tmp", 9 * u + 1, 8 * u + 8), R("cu", 8 * u, 8 * u + 7 - u), R("alg", 9 * u - 8, 9 * u - 7), R("tmp", 9 * u - 8, 9 * u - 7), O.is_ge, O.is_ge)
        tt(R("alg", 9 * u, 8 * u + 8), R("alg", 9 * u - 8, 8 * u), R("tmp", 9 * u - 8, 8 * u), O.min)
        if u < 6:
            both(R("cu", 8 * u + 8, 8 * u + 14 - u), u + 2, u + 1)
        if u == 2:
            ts(R("mk8"), R("nn"), R("ca", 8, 9), None, O.add)
        if u == 6:
            both(R("sl8"), 0, 14)
    al = R("alg", 0, 64, st=9)
    scan(R("cn"), al, al, O.add, O.max)
    tt(R("ck"), R("mk8"), al, O.mult)
    ts(R("ms8"), R("sl8"), R("ca", 8, 9), None, O.add)
    tt(R("z8"), R("cn"), R("ck"), O.add)
    red(R("nlv"), R("z8"), O.min, True)
    ts(R("kl", 0, 1), R("nlv"), 8192.0, R("ca", 4, 5), O.mult, O.min)
    ts(R("own"), R("pm"), R("nlv"), None, O.add)
    ts(R("nls"), R("nlv"), 8192.0, R("ca", 4, 5), O.mult, O.min)
    ttg(R("same"), R("ids"), R("kl", 0, 1), R("own"), O.is_equal)
    tt(R("ms9"), R("ms8"), al, O.mult)
    red(R("dup"), R("same"), O.max)
    tt(R("y8"), R("cn"), R("ms9"), O.add)
    ts(R("kd", 0, 1), R("dup"), R("ca", 4, 5), R("nls"), O.mult, O.max)
    send([(q, R("kd"), R("kla", 2 * here[q], 2 * here[q] + 2)) for q in others], "ark")

    parts = [(ch, b) for ch in range(2) for b in range(4)]
    for ch, b in parts:
        mm(BANKS[4 * ch + b], CUT[ch][1] - CUT[ch][0], "eq", 128 * b, "vq", CUT[ch][0], CUT[ch][1], True, False)
    scatter(R("wo"), R("kd", 0, 1), R("ptv", 16 * r, 16 * r + 16))
    red(R("slv"), R("y8"), O.min, True)
    ts(R("yv"), R("slv"), 0.5, 8192.0, O.is_lt, O.mult)
    turn(R("tko"), R("wo", P * r, P * r + P))
    tt(R("zz", 96, 97), R("slv"), R("yv"), O.mult)
    turn(R("yr"), R("zz", 96, 128))
    tt(R("wown"), R("tko", 0, P, st=32), R("tko", 16, P, st=32), O.min)
    gather(R("yd"), R("yr"), R("hv"))
    turn(R("ydt"), R("yd"))
    for a in range(4):
        for b in range(4):
            copy(R("ksl", 2 * a, 2 * a + 2, 32 * b, 32 * b + 32), R("ydt", 0, 64, 32 * a, 32 * a + 32, 32), "s")

    note(None, [R("kla")], [], "ark", count["ark"])
    for k, q in reversed(list(enumerate(others))):
        scatter(R("wk"), R("kla", 2 * k, 2 * k + 1), R("ptv", 16 * q, 16 * q + 16))
        if k == 2:
            ts(R("kt"), R("nlv"), 0.5, None, O.is_lt)
        if k == 1:
            ts(R("kw"), R("nlv"), 8192.0, 1.0, O.mult, O.add)
    tt(R("kv"), R("kw"), R("kt"), O.mult)
    turn(R("tk"), R("wk", P * r, P * r + P))
    ts(R("zz", 64, 68), R("mk4"), R("kv"), None, O.mult)
    tt(R("wa"), R("tk", 0, P, st=32), R("tk", 16, P, st=32), O.min)
    pick("kq", 0, 64, "uc", UW, R("ksl", 0, 4))
    tt(R("wb"), R("wa"), R("wown"), O.min)
    turn(R("kpt"), R("zz", 64, 96))
    tt(R("wc", 0, 12, 0, 64), R("wb", 0, 12, 0, 64), R("wb", 0, 12, 64, 128), O.min)
    for a in range(4):
        tt(R("zz", 32, 44, 32 * a, 32 * a + 32), R("wc", 0, 12, 0, 32), R("wc", 0, 12, 32, 64), O.min)
    turn(R("lr"), R("zz", 32, 64))
    pick("kq", 64, 128, "uc", UW, R("ksl", 4, 8))
    gather(R("ld"), R("lr"), R("hv"))
    tt(R("kp2"), R("kpt", 0, 32, st=2), R("kpt", 1, 32, st=2), O.add)
    turn(R("ldt"), R("ld"))
    tt(R("kp3"), R("kp2", 0, 16, st=2), R("kp2", 1, 16, st=2), O.add)
    copy(R("ln", 0, 24, st=2), R("ldt", 0, 12))
    copy(R("ln", 1, 24, st=2), R("ldt", 32, 44), "s")
    ts(R("kpo"), R("kp3"), -1.0, None, O.add)
    for a in range(4):
        dma("y", T.kp[:, 8 * a:8 * a + 8], R("kpo", 0, 8, 32 * a, 32 * a + 4), "dk", 4)

    note(None, [R("xa" + s, 32 * q, 32 * q + 32) for q in others for s in ("", "s")], [], "arx", count["arx"])
    for a, b in CUT:
        pick("qp", a, b, "xa", 160, R("ln", a // 16, b // 16))
    for ch, b in parts:
        mm(BANKS[4 * ch + b], CUT[ch][1] - CUT[ch][0], "eq", 128 * b, "qp", CUT[ch][0], CUT[ch][1], False, True)
    ts(R("sl0"), R("ln"), N * A - 0.5, float(P), O.is_lt, O.mult)
    tt(R("sl1"), R("sl0"), R("jc"), O.add)

    def half(ch, bs):
        for b in bs:
            copy(R("nt", 4 * CUT[ch][0] + b, 4 * CUT[ch][1], st=4), R(BANKS[4 * ch + b], 0, CUT[ch][1] - CUT[ch][0]), "sv"[b % 2])

    def new(ch):
        quant("mg", P + CUT[ch][0], P + CUT[ch][1], R("nt", 4 * CUT[ch][0], 4 * CUT[ch][1]))

    def store(ch, late):
        a, b = CUT[ch]
        pick("oq", a, b, "mg", 2 * P, R("sl", a // 16, b // 16))
        dma("y", T.oc[:, 4 * a:4 * b], R("oq", a, b), "do%d" % ch, 1)
        for k in range(4):
            dma("sy"[k % 2] if late else "y", T.osc[4 * k:4 * k + 4, a:b], R("oqs", a, b, 32 * k, 32 * k + 4), "dp%d" % ch, 4)
    half(0, (0, 1))
    copy(R("sl"), R("sl1"))
    half(0, (2, 3))
    mm(BANKS[0], 128, "wq", 0, "kq", 0, 128)
    new(0)
    half(1, (0, 2))
    store(0, False)
    half(1, (1, 3))
    copy(R("yt"), R(BANKS[0], 0, 128), "s")
    dma("y", T.y[:, :], R("yt"), "dy", 1)
    new(1)
    store(1, True)

    for s in sorted(count):
        g.wait_ge(T.sem[s], count[s])
